import numpy as np, ml_dtypes
CORES = [3,7,11,15,131,135,139,143]
N = 8
BF = ml_dtypes.bfloat16
W, Q, TV, HOP, M = 2048, 256, 6, 5, 10
def parts(rng):
    hi = rng.choice(np.array([64, 128, 192, 256]), (N, 8, 1, W)); p = np.floor(hi * rng.random((N, 8, 16, W)))
    lo = rng.choice(np.array([0, 32, 64, 128, 192]), (N, 8, 1, Q)); y = lo + np.floor((256 - lo) * rng.random((N, 8, 16, Q)))
    L = rng.integers(0, W, (N, 8, 16, Q)); share = rng.choice(np.array([0.0, 0.1, 0.3, 0.7, 1.0]), (N, 8, 1, Q))
    C = np.where(rng.random((N, 8, 16, Q)) < share, rng.integers(0, W, (N, 8, 16, Q)), -1)
    o = rng.integers(0, 16, (N, 8, 16, Q)); b = np.minimum(rng.integers(0, 8, (N, 8, 16, Q)), rng.integers(0, 8, (N, 8, 16, Q)))
    return p, y, L, C, o, b, rng.integers(0, 4, (N, 8, 16, TV))
def pack(p, y, L, C, o, b, lim):
    def half(a): return np.ascontiguousarray(np.asarray(a, np.float32).reshape(N, 128, -1)).astype(BF)
    def whole(a): return np.ascontiguousarray(np.asarray(a).reshape(N, 128, -1)).astype(np.int32)
    return {"prop": half(p), "lem": whole(L), "con": whole(C), "org": half(o), "cnt": half(b), "ex": half(y), "lim": whole(lim)}
def setup_inputs(rng):
    return pack(*parts(rng))
def setup_inputs_spread(rng):
    p, y, L, C, o, b, lim = parts(rng)
    p = np.minimum(np.floor(np.exp2(8 * rng.random((N, 8, 1, W))) * rng.random((N, 8, 16, W))), 255)
    y = np.minimum(np.floor(np.exp2(2 + 6 * rng.random((N, 8, 1, Q))) * rng.random((N, 8, 16, Q))), 255)
    y = np.where(rng.random((N, 8, 1, Q)) < 0.5, 255 - y, y)
    L = np.minimum(np.floor(W * rng.random((N, 8, 16, Q)) ** 3), W - 1)
    C = np.where(C >= 0, W - 1 - np.minimum(np.floor(W * rng.random((N, 8, 16, Q)) ** 3), W - 1), -1)
    o = np.minimum(np.floor(16 * rng.random((N, 8, 16, Q)) ** 2), 15); b = rng.integers(0, 8, (N, 8, 16, Q))
    return pack(p, y, L, C, o, b, lim)
def setup_inputs_ends(rng):
    p = 255 * (rng.random((N, 8, 16, W)) < rng.choice(np.array([0.0, 0.5, 1.0]), (N, 8, 1, W))).astype(np.int64)
    y = 255 * (rng.random((N, 8, 16, Q)) < rng.choice(np.array([0.0, 0.5, 1.0]), (N, 8, 1, Q))).astype(np.int64)
    just = np.argsort(rng.random((N, 8, 16, Q)), axis=2) < 16 - M
    y = np.where(rng.random((N, 8, 1, Q)) < 0.25, 255 * just, y)
    L = (W - 1) * rng.integers(0, 2, (N, 8, 16, Q)); share = rng.choice(np.array([0.0, 0.5, 1.0]), (N, 8, 1, Q))
    C = np.where(rng.random((N, 8, 16, Q)) < share, W - 1, -1)
    o = 15 * rng.integers(0, 2, (N, 8, 16, Q)); b = 7 * rng.integers(0, 2, (N, 8, 16, Q)); lim = 3 * rng.integers(0, 2, (N, 8, 16, TV))
    turn = int(rng.integers(0, 4))
    for r in range(N):
        for g in range(8):
            w = (r + g + turn) % 4
            if (r, g) in ((0, 0), (N - 1, 7)): w = 3
            if (r, g) in ((0, 7), (N - 1, 6)): w = 1
            pm = rng.permutation(16)
            p[r, g, :, 0] = (0 * pm, 0 * pm + 255, 255 * (pm < M), 0 * pm)[w]
            p[r, g, :, W - 1] = (0 * pm + 255, 0 * pm, 255 * (pm < M - 1), 0 * pm)[w]
            for c in (0, Q - 1):
                if w == 3: y[r, g, :, c] = 255
                if w == 1:
                    y[r, g, :, c] = 0; L[r, g, :, c] = W - 1; L[r, g, 15, c] = 0; C[r, g, :, c] = W - 1; C[r, g, 15, c] = -1
                if w == 0:
                    y[r, g, :, c] = 254 + (pm < 16 - M); L[r, g, :, c] = 0; L[r, g, 15, c] = W - 1; C[r, g, :, c] = 0
    return pack(p, y, L, C, o, b, lim)
def setup_inputs_corners(rng):
    p, y, L, C, o, b, lim = parts(rng)
    p[..., :W // 4] = np.floor(0.125 * p[..., :W // 4]); p[..., W // 2:] = 96 + np.floor(160 * rng.random((N, 8, 16, W - W // 2))); p[..., W - 1] = 255
    y = 32 + np.floor(224 * rng.random((N, 8, 16, Q))); y = np.where(rng.random((N, 8, 1, Q)) < 0.125, 255, y)
    e = (np.arange(Q).reshape(1, 1, 1, Q) + rng.integers(0, 6, (N, 8, 1, 1))) % 6; k = np.arange(16).reshape(1, 1, 16, 1)
    name = np.where(rng.random((N, 8, 1, Q)) < 0.6, rng.integers(0, W // 4, (N, 8, 16, Q)), rng.integers(0, W, (N, 8, 16, Q)))
    hole = rng.choice(np.array([0, 15, 15, 6]), (N, 8, 1, Q))
    has = np.where(e == 0, False, np.where(e == 2, k != hole, np.where(e == 3, k == 15, True)))
    C = np.where(has, name, -1)
    L = np.where(rng.random((N, 8, 1, Q)) < 0.5, rng.integers(W // 2, W, (N, 8, 16, Q)), L)
    mode = rng.integers(0, 4, (N, 8, 1, Q)); o = np.where(mode == 0, k, np.where(mode == 1, 0, np.where(mode == 2, 15, o)))
    b = rng.choice(np.array([0, 0, 1, 3, 6, 7]), (N, 8, 16, Q)); b = np.where(e == 4, 7, np.where(e == 5, 7 * (k == 15), b))
    lim = 3 * rng.integers(0, 2, (N, 8, 16, TV))
    for c in (Q - 2, Q - 1):
        y[:, :, :, c] = 0; C[:, :, :, c] = -1; C[:, :, 15, c] = W - 1; b[:, :, 15, c] = 0
    y[:, 0, :, Q - 2] = 255; C[:, 0, :, Q - 2] = -1
    return pack(p, y, L, C, o, b, lim)
def setup_inputs_ties(rng):
    p, y, L, C, o, b, lim = parts(rng)
    base = rng.integers(2, 254, (1, 8, 16, 1))
    m = np.where(rng.random((N, 8, 1, W)) < 0.06, M + rng.integers(0, 2, (N, 8, 1, W)), rng.choice(np.array([M - 1, M - 1, M - 2, 0]), (N, 8, 1, W)))
    up = np.argsort(rng.random((N, 8, 16, W)), axis=2) < m
    p = base + np.where(m == 0, 0, np.where(up, 1, 0 - rng.integers(0, 2, (N, 8, 16, W))))
    y = base + np.where(rng.random((N, 8, 1, Q)) < 0.6, 0, rng.integers(-1, 2, (N, 8, 16, Q)))
    b = rng.integers(0, 3, (N, 8, 16, Q))
    p[..., :80] = (np.arange(80).reshape(1, 80) + np.arange(16).reshape(16, 1)) >> 4
    y[..., Q - 16:] = 255; L[..., Q - 16:] = rng.integers(0, 80, (N, 8, 16, 16)); L[..., Q - 8:] = rng.integers(0, 2, (N, 8, 16, 8))
    L[:, :, 0, Q - 16:] = 0; L[:, :, 15, Q - 8:] = 1
    us = np.arange(2048, 4081 - M).reshape(-1, 1); names = np.arange(2048, W).reshape(1, -1); x = us * names
    iu, ia = np.nonzero(((x & 63) == 32) & (x > 2 ** 23) & ((((x >> 5) + names + 97) & 255) == 0) & ((names & 255) < Q - 16))
    if len(iu) > 0:
        for g in range(8):
            s = int(rng.integers(0, len(iu))); u = int(us[iu[s], 0]); a = int(names[0, ia[s]]); c = a & 255
            p[:, g, :, a] = 255; y[:, g, :, c] = (u + np.argsort(rng.random((N, 16)), axis=1)) >> 4
            C[:, g, :, c] = -1; C[:, g, 0, c] = a; o[:, g, 0, c] = 0; b[:, g, 0, c] = 7
    return pack(p, y, L, C, o, b, lim)
def setup_inputs_alike(rng):
    p, y, L, C, o, b, lim = parts(rng); c = np.arange(Q).reshape(1, 1, 1, Q)
    few = np.array([0, W - 1, W // 2, 3])
    L[:, 0::4] = rng.choice(few, (N, 2, 16, Q))
    L[:, 1::4] = np.repeat(L[:, 1::4, :1], 16, axis=2)
    L[:, 2::4] = 256 * rng.integers(0, W // 256, (N, 2, 16, Q)) + c
    L[:, 3::4] = 256 * rng.integers(0, W // 256, (N, 2, 16, Q)) + (c + 1) % Q
    own = rng.random((N, 8, 1, Q)) < 0.5
    C = np.where((C >= 0) & own, L[:, :, ::-1], C); b[:, ::2] = 2
    return pack(p, y, L, C, o, b, lim)
def check_inputs(d):
    bad = []
    for k, lo, hi in (("prop", 0, 255), ("lem", 0, W - 1), ("con", -1, W - 1), ("org", 0, 15), ("cnt", 0, 7), ("ex", 0, 255), ("lim", 0, 3)):
        a = np.asarray(d[k]).astype(np.float64)
        if not (np.min(a) >= lo and np.max(a) <= hi): bad.append("range of " + k)
        elif not np.all(a == np.floor(a)): bad.append("whole numbers in " + k)
    return bad
def pick(p, a):
    return np.take_along_axis(p, a.reshape(N, 8, 1, 16 * Q), 3).reshape(N, 8, 16, 16, Q)
def at(a, k):
    return np.take_along_axis(a, k[:, :, None, :], 2)[:, :, 0]
def reference(prop, lem, con, org, cnt, ex, lim):
    p = prop.astype(np.float32).astype(np.int16).reshape(N, 8, 16, W); y = ex.astype(np.float32).astype(np.int16).reshape(N, 8, 16, Q)
    L = lem.astype(np.int64).reshape(N, 8, 16, Q); C = con.astype(np.int64).reshape(N, 8, 16, Q)
    o = org.astype(np.float32).astype(np.int64).reshape(N, 8, 16, Q); b = cnt.astype(np.float32).astype(np.int64).reshape(N, 8, 16, Q)
    lm = lim.astype(np.int64).reshape(N, 8, 16, TV); w = np.zeros((N, Q), np.int64)
    rows = np.arange(16).reshape(1, 1, 16, 1); lane = np.arange(Q).reshape(1, 1, Q)
    for t in range(TV):
        y5 = y[:, :, :, None, :]; pl = pick(p, L); pc = pick(p, np.maximum(C, 0))
        bar = (np.add.reduce(pc > y5, axis=2, dtype=np.int64) >= M) & (C >= 0)
        gui = np.add.reduce(pl > y5, axis=2, dtype=np.int64) >= M
        score = np.add.reduce(np.abs(pl - y5), axis=2, dtype=np.int64); u = np.add.reduce(y, axis=2, dtype=np.int64)
        barred = np.any(bar, axis=2); some = np.any(gui, axis=2); guilty = ~barred & some; clear = ~barred & ~some
        kb = np.argmax(bar, axis=2); hit = barred[:, :, None] & (rows == kb[:, :, None]); b1 = b + hit
        over = hit & (b1 > lm[:, :, :, t:t + 1] + w[:, None, None, :]); back = np.any(over, axis=2)
        L1 = np.where(back[:, :, None] & (rows == at(o, kb)[:, :, None]), at(C, kb)[:, :, None], L)
        C1 = np.where(over, -1, C); b1 = np.where(over, 0, b1)
        kg = np.argmax(gui, axis=2); old = at(L, kg); empty = C < 0
        slot = np.where(np.any(empty, axis=2), np.argmax(empty, axis=2), np.argmax(b, axis=2)); put = guilty[:, :, None] & (rows == slot[:, :, None])
        n = ((((u * old) >> 5) + old + 97 * t) & (W - 256)) + lane
        C1 = np.where(put, old[:, :, None], C1); o1 = np.where(put, kg[:, :, None], o); b1 = np.where(put, 0, b1)
        L1 = np.where(guilty[:, :, None] & (rows == kg[:, :, None]), n[:, :, None], L1)
        pv = np.take_along_axis(pl, kg[:, :, None, None, :], 3)[:, :, :, 0]
        np.put_along_axis(p, n[:, :, None, :], np.where(guilty[:, :, None], np.minimum(pv, y), np.take_along_axis(p, n[:, :, None, :], 3)), 3)
        y = np.where(guilty[:, :, None], np.abs(y - pv), y)
        ks = np.argmin(score, axis=2); new = (((u * u) >> 5) + 37 * u + t) & (W - 1)
        L1 = np.where(clear[:, :, None] & (rows == ks[:, :, None]), new[:, :, None], L1)
        w = np.add.reduce(barred, axis=1, dtype=np.int64) & 3
        L, C, o, b = L1, C1, o1, b1
        if t < TV - 1: L, C, o, b = [np.roll(a, HOP, axis=0) for a in (L, C, o, b)]
    def half(a): return a.reshape(N, 128, -1).astype(np.float32).astype(BF)
    return {"zp": half(p), "zl": L.reshape(N, 128, Q).astype(np.float32), "zc": C.reshape(N, 128, Q).astype(np.float32), "zo": half(o), "zb": half(b), "zy": half(y)}

@@ -1,0 +1,522 @@
+from concourse.mybir import AluOpType as A, ActivationFunctionType as AF, AxisListType as AX
+
+TV, HOP = 6, 5
+BIG = float(2 ** 25)
+CAP = float(2 ** 24)
+W = 256
+SCRATCH = {
+    "P": ("sbuf", [128, 4352], "bfloat16"), "NID": ("sbuf", [128, 128], "bfloat16"),
+    "PC": ("sbuf", [128, 16, 256], "bfloat16"), "PL": ("sbuf", [128, 16, 256], "bfloat16"),
+    "XC": ("sbuf", [128, 16, 256], "bfloat16"), "XL": ("sbuf", [128, 16, 256], "bfloat16"),
+    "DL": ("sbuf", [128, 16, 256], "bfloat16"), "AB": ("sbuf", [128, 16, 256], "bfloat16"),
+    "yv": ("sbuf", [128, 256], "bfloat16"), "dv": ("sbuf", [128, 256], "bfloat16"), "mn": ("sbuf", [128, 256], "bfloat16"),
+    "C16": ("sbuf", [128, 256 * TV], "uint16"), "L16": ("sbuf", [128, 256 * TV], "uint16"),
+    "PK": ("sbuf", [128, 256 * TV], "int32"), "LK": ("sbuf", [128, 256 * TV], "int32"),
+    "oC16": ("sbuf", [128, 256 * TV], "uint16"), "oL16": ("sbuf", [128, 256 * TV], "uint16"),
+    "oPK": ("sbuf", [128, 256 * TV], "int32"), "oLK": ("sbuf", [128, 256 * TV], "int32"),
+    "lemA": ("sbuf", [128, 256], "int32"), "conA": ("sbuf", [128, 256], "int32"), "limA": ("sbuf", [128, TV], "int32"),
+    "orgA": ("sbuf", [128, 256], "bfloat16"), "cntA": ("sbuf", [128, 256], "bfloat16"),
+    "f0": ("sbuf", [128, 256], "float32"), "f1": ("sbuf", [128, 256], "float32"), "f2": ("sbuf", [128, 256], "float32"),
+    "f3": ("sbuf", [128, 256], "float32"), "f4": ("sbuf", [128, 256], "float32"), "zPK": ("sbuf", [128, 256], "float32"), "zLK": ("sbuf", [128, 256], "float32"),
+    "i0": ("sbuf", [128, 256], "int32"), "i1": ("sbuf", [128, 256], "int32"),
+    "i2": ("sbuf", [128, 256], "int32"), "h0": ("sbuf", [128, 256], "bfloat16"), "h1": ("sbuf", [128, 256], "bfloat16"),
+    "KC": ("sbuf", [128, 256], "float32"), "key": ("sbuf", [128, 256], "float32"),
+    "keyS": ("sbuf", [128, 256], "float32"), "SS": ("sbuf", [128, 256], "float32"),
+    "SB": ("sbuf", [128, 256], "float32"), "SG": ("sbuf", [128, 256], "float32"), "SC": ("sbuf", [128, 256], "float32"),
+    "RC": ("sbuf", [128, 256], "bfloat16"), "RL": ("sbuf", [128, 256], "bfloat16"),
+    "eC": ("sbuf", [128, 256], "bfloat16"), "eL": ("sbuf", [128, 256], "bfloat16"),
+    "EVC": ("sbuf", [128, 256], "float32"), "EVL": ("sbuf", [128, 256], "float32"),
+    "ERC": ("sbuf", [128, 256], "bfloat16"), "ERL": ("sbuf", [128, 256], "bfloat16"),
+    "Yp": ("sbuf", [128, 16, 32], "float32"), "Yl": ("sbuf", [128, 16, 32], "float32"), "Z": ("sbuf", [128, 16, 32], "float32"),
+    "ones": ("sbuf", [128, 256], "bfloat16"), "ID": ("sbuf", [128, 128], "bfloat16"), "BT": ("sbuf", [128, 128], "bfloat16"),
+    "BLK": ("sbuf", [128, 128], "bfloat16"), "RK": ("sbuf", [128, 256], "bfloat16"), "mt": ("sbuf", [128, 128], "bfloat16"),
+    "SELC": ("sbuf", [128, 2048], "bfloat16"), "SELS": ("sbuf", [128, 2048], "bfloat16"),
+    "THR": ("sbuf", [128, 256], "bfloat16"), "KI": ("sbuf", [128, 256], "float32"), "KB": ("sbuf", [128, 256], "bfloat16"),
+    "D0": ("sbuf", [128, 256], "float32"), "D1": ("sbuf", [128, 256], "float32"), "D1h": ("sbuf", [128, 256], "bfloat16"),
+    "fb": ("sbuf", [128, 256], "float32"), "RLM": ("sbuf", [128, 256 * TV], "bfloat16"), "limf": ("sbuf", [128, TV], "float32"),
+    "col": ("sbuf", [128, 8], "float32"), "cb": ("sbuf", [128, 16], "float32"), "kq": ("sbuf", [128, 16], "float32"),
+    "LF": ("sbuf", [128, 16 * 64], "float32"), "LI": ("sbuf", [128, 16 * 64], "int32"), "bfl": ("sbuf", [128, 16], "bfloat16"),
+    "U16": ("sbuf", [128, 32], "uint16"),
+    "pC": ("psum", [128, 512], "float32"), "pL": ("psum", [128, 512], "float32"), "pS": ("psum", [128, 512], "float32"),
+    "pM": ("psum", [128, 512], "float32"), "pY": ("psum", [128, 32, 16], "float32"), "pT": ("psum", [128, 512], "float32"),
+    "pD0": ("psum", [128, 16, 32], "float32"), "pD1": ("psum", [128, 16, 32], "float32"),
+}
+_LOADS = ["prop", "lem", "con", "ex", "lim", "org", "cnt"]
+_KINDS = ["C16", "PK", "L16", "LK"]
+SEMAPHORES = (["qV", "qS", "qP", "qG", "sent", "outs"] + ["ld_" + n for n in _LOADS]
+              + ["a%s_%d" % (k, t) for k in _KINDS for t in range(1, TV)])
+
+
+def rank_program(g, core, T, topo):
+    rank = T.rank_of(core)
+    if rank is None:
+        return
+    eng = {"V": g.vector, "S": g.scalar, "P": g.tensor, "G": g, "Y": g.sync}
+    cnt = {}
+    seen = {q: {} for q in eng}
+    snap = {}
+    wrote, read = {}, {}
+
+    def require(q, dep):
+        s, n = dep
+        if seen[q].get(s, 0) >= n:
+            return
+        eng[q].wait_ge(T.sem[s], n)
+        for a, b in list(snap.get(dep, {}).items()) + [dep]:
+            if seen[q].get(a, 0) < b:
+                seen[q][a] = b
+
+    def order(q, reads, writes):
+        deps = {}
+        for t in reads + writes:
+            for s, n in wrote.get(t, []):
+                deps[s] = max(deps.get(s, 0), n)
+        for t in writes:
+            for s, n in read.get(t, {}).values():
+                deps[s] = max(deps.get(s, 0), n)
+        own = "q" + q
+        for s in sorted(deps, key=lambda s: s == own):
+            require(q, (s, deps[s]))
+
+    def note(q, reads, writes, dep):
+        snap[dep] = dict(seen[q])
+        for t in reads:
+            read.setdefault(t, {})[q] = dep
+        for t in writes:
+            wrote[t] = [dep]
+            read[t] = {}
+
+    banks = {"pC", "pL", "pS", "pM", "pY", "pT", "pD0", "pD1"}
+    bank_use = {}
+
+    def do(q, reads, writes, calls):
+        order(q, reads, writes)
+        used = {t.split(":")[0] for t in reads + writes} & banks
+        for b in sorted(used):
+            for qq, dep in bank_use.get(b, {}).items():
+                if qq != q:
+                    require(q, dep)
+        s = "q" + q
+        for c in calls:
+            c().then_inc(T.sem[s], 1)
+            cnt[s] = cnt.get(s, 0) + 1
+        note(q, reads, writes, (s, cnt[s]))
+        for b in used:
+            bank_use.setdefault(b, {})[q] = (s, cnt[s])
+
+    def X(name, idx=None, tok=None):
+        return (T[name][:] if idx is None else T[name][idx], tok or name)
+
+    def cols(name, a, b, tok=None):
+        return X(name, (slice(None), slice(a, b)), tok)
+
+    lanes = {"LF": {}, "LI": {}}
+
+    def lane(buf, n):
+        j = lanes[buf].setdefault(n, len(lanes[buf]))
+        return cols(buf, 16 * j, 16 * j + 16, buf + ":" + n)
+
+    def F(n):
+        return lane("LF", n)
+
+    def I(n):
+        return lane("LI", n)
+
+    def first(name):
+        return X(name, (slice(None), slice(0, 256, 16)))
+
+    def final(name):
+        return X(name, (slice(None), slice(15, 256, 16)))
+
+    v, s_, p = g.vector, g.scalar, g.tensor
+
+    def tt(o, a, b, op):
+        do("V", [a[1], b[1]], [o[1]], [lambda: v.tensor_tensor(out=o[0], in0=a[0], in1=b[0], op=op)])
+
+    def ts(o, a, s1, op0, s2=None, op1=None, extra=()):
+        kw = {"op1": op1} if op1 is not None else {}
+        do("V", [a[1]] + list(extra), [o[1]],
+           [lambda: v.tensor_scalar(out=o[0], in0=a[0], scalar1=s1, scalar2=s2, op0=op0, **kw)])
+
+    def cp(o, a):
+        do("V", [a[1]], [o[1]], [lambda: v.tensor_copy(out=o[0], in_=a[0])])
+
+    def fill(o, c):
+        do("V", [], [o[1]], [lambda: v.memset(o[0], c)])
+
+    def scan(o, d0, d1, op0, op1):
+        do("V", [d0[1], d1[1]], [o[1]], [lambda: v.tensor_tensor_scan(out=o[0], data0=d0[0], data1=d1[0], initial=0.0, op0=op0, op1=op1)])
+
+    def act(o, a, func, scale=1.0, extra=()):
+        do("S", [a[1]] + list(extra), [o[1]], [lambda: s_.activation(out=o[0], in_=a[0], func=func, scale=scale)])
+
+    def mm(o, pairs):
+        reads = [t[1] for pr in pairs for t in pr]
+        n = len(pairs)
+        do("P", reads, [o[1]], [(lambda i=i, l=l, r=r: p.matmul(o[0], l[0], r[0], i == 0, i == n - 1)) for i, (l, r) in enumerate(pairs)])
+
+    SHR, AND = A.logical_shift_right, A.bitwise_and
+
+    def load(q, name, dst):
+        s = "ld_" + name
+        eng[q].dma_start(dst[0], T[name][:]).then_inc(T.sem[s], 16)
+        cnt[s] = 16
+        note(q, [], [dst[1]], (s, 16))
+    load("Y", "con", X("conA"))
+    load("S", "prop", cols("P", 0, 2048))
+    load("Y", "ex", X("yv"))
+    load("Y", "lem", X("lemA"))
+    load("Y", "org", X("orgA"))
+    load("Y", "cnt", X("cntA"))
+    load("Y", "lim", X("limA"))
+
+    def sel(o, a, pat, cmp, fillv, base, cm):
+        do("G", [a[1]], [o[1]], [lambda: g.affine_select(o[0], a[0], pat, cmp, fillv, base, cm)])
+
+    def iota(o, pat, base, cm):
+        do("G", [], [o[1]], [lambda: g.iota(o[0], pat, base, cm, allow_small_or_imprecise_dtypes=True)])
+    fill(X("ones"), 1.0)
+    one128 = cols("ones", 0, 128)
+    sel(X("ID"), one128, [[-1, 128]], A.is_equal, 0.0, 0, 1)
+    sel(X("BT"), one128, [[-16, 8], [0, 16]], A.is_ge, 0.0, 0, 1)
+    sel(X("BLK"), X("BT"), [[16, 8], [0, 16]], A.is_ge, 0.0, 15, -1)
+    fill(cols("P", 2048, 2304, "Pz"), 0.0)
+    fill(X("THR"), 9.5 * BIG)
+    fill(X("SELC"), 0.0)
+    fill(X("EVC"), 0.0)
+    fill(X("EVL"), 0.0)
+    fill(X("ERC"), -1.0)
+    fill(X("ERL"), -1.0)
+    fill(X("fb"), -float(2 ** 30))
+    fill(X("SC"), 1.0)
+    fill(I("w"), 0)
+    emp = X("f0")
+    ts(emp, X("conA"), 0.0, A.is_lt)
+    ts(X("f1"), emp, 2049.0, A.mult)
+    tt(X("f1"), X("f1"), X("conA"), A.add)
+    cp(cols("C16", 0, 256, "C16_0"), X("f1"))
+    mm(X("pY", (slice(None), slice(0, 16))), [(X("ID"), X("yv"))])
+    cp(cols("L16", 0, 256, "L16_0"), X("lemA"))
+    for i in range(16):
+        b8 = X("BLK", (slice(None), slice(0, 128, 16)))
+        ts(X("SELC", (slice(None), slice(129 * i, 128 * i + 128, 16))), b8, -BIG, A.mult)
+
+    def selq(nm, q):
+        return cols(nm, 128 * q, 128 * q + 128, nm)
+    yr = [X("yv", (slice(None), slice(q, 256, 16))) for q in range(16)]
+
+    def gather(t, lst, dst, m, q="S"):
+        tok = "%s_%d" % (lst, t)
+        win = T.P[:, 0:2064].indirect(T[lst][:, 256 * t + 16 * m:256 * t + 16 * m + 16])
+        out = T[dst][:, m, :]
+        do(q, [tok, "P", "Pz"], ["%s:%d" % (dst, m)],
+           [(lambda: s_.activation(out=out, in_=win, func=AF.Copy)) if q == "S" else (lambda: v.tensor_copy(out=out, in_=win))])
+
+    def rows_of(t, k):
+        return slice(k, 256, 16) if t == 0 else slice(16 * k, 16 * k + 16)
+
+    def lanes_of(t, q):
+        return slice(16 * q, 16 * q + 16) if t == 0 else slice(q, 256, 16)
+
+    def toks(b, m0, m1):
+        return ["%s:%d" % (b, m) for m in range(m0, m1)]
+
+    def compare(t, src, dst, op, m0, m1):
+        ms = slice(m0, m1)
+        do("V", toks(src, m0, m1) + ["pY"], toks(dst, m0, m1),
+           [(lambda k=k: v.tensor_tensor(out=T[dst][:, ms, rows_of(t, k)], in0=T[src][:, ms, rows_of(t, k)], in1=T.pY[:, ms, :], op=op))
+            for k in range(16)])
+
+    def sums(t, src, bank, sl, const, m0, m1, made=None):
+        ms, cs = slice(m0, m1), slice(16 * m0, 16 * m1)
+        out = T[bank][:, cs]
+        calls = [lambda: p.matmul(out, T.ID[:], T[const][:, cs], True, False)]
+        calls += [(lambda q=q: p.matmul(out, T[sl][:, 128 * q:128 * q + 128], T[src][:, ms, lanes_of(t, q)], False, q == 15)) for q in range(16)]
+        do("P", ["ID", const, sl] + (made or toks(src, m0, m1)), ["%s:%d" % (bank, m) for m in range(m0, m1)], calls)
+
+    def whole(bank):
+        return [("%s:%d" % (bank, m)) for m in range(16)]
+
+    def keyed(o, bank, b):
+        do("V", whole(bank) + [b[1]], [o[1]], [lambda: v.tensor_tensor(out=o[0], in0=T[bank][:, 0:256], in1=b[0], op=A.max)])
+
+    cpieces = [(0, 8), (8, 16)]
+    HB = 4
+    lpieces = [(0, 4), (4, 8), (8, 12), (12, 16)]
+    VG = 3
+    dst = T.cores[(rank + HOP) % len(T.cores)]
+    rid, pid = topo.addr(dst, core)
+    msk = topo.mask(core, dst)
+    neng = len(topo.engines(core, dst))
+    sent = [0]
+
+    def send(kind, t):
+        c = slice(256 * t, 256 * t + 256)
+        d = slice(256 * t + 256, 256 * t + 512)
+        order("G", ["o%s_%d" % (kind, t)], [])
+        g.remote_dma(T[kind][:, d], T["o" + kind][:, c], T.sem["a%s_%d" % (kind, t + 1)], T.sem.sent, pid, rid, msk)
+        sent[0] += neng
+
+    def masks(src, y):
+        for e in range(2):
+            act(X(y, (slice(None), slice(None), slice(16 * e, 16 * e + 16)), "%s%d" % (y, e)), src, AF.Copy, T.col[:, e:e + 1], extra=["col"])
+
+    def turn(y, dst):
+        do("V", [y + "0", y + "1"], ["Z"], [(lambda m=m: v.transpose(out=T.Z[:, m, :], in_=T[y][:, m, :])) for m in range(16)])
+        tt(dst, X("Z", (slice(None), slice(None), slice(0, 16))), X("Z", (slice(None), slice(None), slice(16, 32))), A.add)
+
+    def consts():
+        tt(cols("mt", 0, 64), cols("ID", 0, 64), cols("ID", 64, 128), A.add)
+        tt(cols("mt", 64, 96), cols("mt", 0, 32), cols("mt", 32, 64), A.add)
+        tt(cols("RK", 0, 16), cols("mt", 64, 80), cols("mt", 80, 96), A.add)
+        for w in (16, 32, 64, 128):
+            cp(cols("RK", w, 2 * w), cols("RK", 0, w))
+        tt(X("kq"), cols("RK", 0, 16), cols("KI", 0, 16), A.mult)
+        do("V", ["kq"], ["col"], [lambda: v.tensor_reduce(out=T.col[:, 2:3], in_=T.kq[:], axis=AX.X, op=A.add)])
+        do("V", ["BLK"], ["col"], [lambda: v.tensor_reduce(out=T.col[:, 0:1], in_=T.BLK[:, 0:128:32], axis=AX.X, op=A.add)])
+        ts(X("col", (slice(None), slice(1, 2))), X("col", (slice(None), slice(0, 1))), -1.0, A.mult, 1.0, A.add)
+        ts(X("col", (slice(None), slice(3, 4))), X("col", (slice(None), slice(2, 3))), float(2 ** 20), A.mult)
+        ts(X("col", (slice(None), slice(4, 5))), X("col", (slice(None), slice(2, 3))), 65536.0, A.mult, 65536.0, A.add)
+        ts(X("cb"), X("cb"), T.col[:, 2:3], A.add, extra=["col"])
+        ts(X("pY", (slice(None), slice(16, 32)), "pY:k"), X("KI"), 0.0625, A.mult)
+        ts(X("NID"), X("ID"), -1.0, A.mult)
+        cp(X("D1h"), X("D1"))
+        ts(X("limf"), X("limA"), 16384.0, A.mult)
+
+    def pack():
+        ts(X("f2"), X("f1"), 8.0, A.mult, T.col[:, 3:4], A.add, extra=["col"])
+        ts(X("f4"), X("orgA"), 65536.0, A.mult)
+        ts(X("f3"), emp, 7.0, A.mult, 1.0, A.add)
+        tt(X("f2"), X("f2"), X("f4"), A.add)
+        tt(X("f4"), X("f3"), X("cntA"), A.mult)
+        ts(X("f3"), X("lemA"), 8.0, A.mult, T.col[:, 4:5], A.add, extra=["col"])
+        tt(X("f2"), X("f2"), X("f4"), A.add)
+
+    iota(cols("KI", 0, 256), [[0, 16], [1, 16]], 0, 0)
+    iota(X("KB"), [[0, 16], [1, 16]], 0, 0)
+    iota(X("cb"), [[16, 16]], 0, 0)
+    sel(X("D0"), X("fb"), [[0, 16], [1, 16]], A.is_gt, float(2 ** 30), 0, 0)
+    sel(X("D1"), X("SC"), [[0, 16], [1, 16]], A.is_gt, 0.0, 0, 0)
+
+    def u_sum():
+        mm(cols("pM", 0, 16, "pM:u"), [(selq("SELS", q), yr[q]) for q in range(16)])
+        act(F("u"), cols("pM", 0, 16, "pM:u"), AF.Copy, 1.0 / 16)
+        act(F("u32"), cols("pM", 0, 16, "pM:u"), AF.Copy, 1.0 / 512)
+
+    def update(tag, e_row, e_val, R, e, old, new):
+        pa, pb = cols("pT", 0, 256, "pT:a"), cols("pT", 256, 512, "pT:b")
+        scan(X(R), X("D1h"), X(e_row), A.mult, A.add)
+        scan(pa, X("D1"), X(e_val), A.mult, A.add)
+        ts(X(e), X(R), 1.0, A.is_equal)
+        tt(pb, pa, old, A.subtract)
+        tt(pa, pb, X(e), A.mult)
+        tt(new, pa, old, A.add)
+
+    stores = [0]
+
+    def store(q, name, src):
+        order(q, [src[1]], [])
+        eng[q].dma_start(T[name][:], src[0]).then_inc(T.sem.outs, 16)
+        stores[0] += 16
+
+    for t in range(TV):
+        last = t == TV - 1
+        c0, c1 = 256 * t, 256 * t + 256
+        pk, lk = cols("PK", c0, c1, "PK_%d" % t), cols("LK", c0, c1, "LK_%d" % t)
+        opk, olk = cols("oPK", c0, c1, "oPK_%d" % t), cols("oLK", c0, c1, "oLK_%d" % t)
+        if last:
+            opk, olk = X("zPK"), X("zLK")
+        if t:
+            for k in _KINDS:
+                dep = ("a%s_%d" % (k, t), neng)
+                wrote["%s_%d" % (k, t)] = [dep]
+        if t == 0:
+            consts()
+            ts(cols("RLM", 0, 256, "RLM_0"), X("RK"), T.limf[:, 0:1], A.mult, extra=["limf"])
+        for m in range(16):
+            gather(t, "C16", "PC", m, "V" if m < VG else "S")
+        def conditions(m0, m1):
+            compare(t, "PC", "XC", A.is_gt, m0, m1)
+            sums(t, "XC", "pC", "SELC", "THR", m0, m1)
+
+        def lemma(m0, m1):
+            if m0 < HB:
+                compare(t, "PL", "DL", A.subtract, m0, m1)
+                do("V", toks("DL", m0, m1), toks("XL", m0, m1),
+                   [lambda: v.tensor_scalar(out=T.XL[:, m0:m1, :], in0=T.DL[:, m0:m1, :], scalar1=0.0, scalar2=None, op0=A.is_gt)])
+            else:
+                compare(t, "PL", "XL", A.is_gt, m0, m1)
+            sums(t, "XL", "pL", "SELC", "THR", m0, m1)
+        for m in range(16 if t else 8):
+            gather(t, "L16", "PL", m)
+        if t == 0:
+            conditions(*cpieces[0])
+            pack()
+            masks(X("f2"), "Yp")
+            masks(X("f3"), "Yl")
+            for m in range(8, 16):
+                gather(t, "L16", "PL", m)
+            act(X("SELS"), X("SELC"), AF.Copy, -16.0 / BIG)
+            conditions(*cpieces[1])
+            turn("Yp", cols("PK", 0, 256, "PK_0"))
+            lemma(*lpieces[0])
+            turn("Yl", cols("LK", 0, 256, "LK_0"))
+            lemma(*lpieces[1])
+            u_sum()
+        lp = cols("pM", 256, 512, "pM:l")
+        mm(lp, [(X("BLK"), cols("RLM", c0, c1, "RLM_%d" % t))])
+        x, sl = X("i0"), I("sl")
+        ts(x, pk, 0x4007, AND)
+        tt(X("KC"), lp, pk, A.add)
+        tt(X("keyS"), X("pY", (slice(None), slice(16, 32)), "pY:k"), x, A.subtract)
+        scan(X("SS"), X("D0"), X("keyS"), A.max, A.min)
+        ts(sl, final("SS"), 16.0, A.mult)
+        ts(sl, sl, 15, AND)
+        ts(F("sP"), sl, float(2 ** 20), A.mult, -65536.0, A.add)
+        ts(F("s1"), sl, 1.0, A.add)
+        if t:
+            for m0, m1 in cpieces:
+                conditions(m0, m1)
+            lemma(*lpieces[0])
+        keyed(X("key"), "pC", X("KC"))
+        scan(X("SB"), X("D0"), X("key"), A.max, A.min)
+        mb, mi = final("SB"), I("mi")
+        ts(X("bfl"), mb, CAP, A.is_lt)
+        ts(mi, mb, CAP - 1, A.min)
+        ts(F("thr"), X("bfl"), -CAP, A.mult, CAP, A.add)
+        ts(I("lim"), mi, 14, SHR, 3, AND)
+        ts(I("b"), mi, 7, AND)
+        ts(I("kb"), mi, 20, SHR)
+        ts(I("t2"), mi, 0x3FFF, AND)
+        tt(F("bl"), I("b"), I("lim"), A.subtract)
+        ts(I("t1"), mi, 0xFF0000, AND)
+        tt(F("ov"), F("bl"), I("w"), A.is_ge)
+        ts(F("kb1"), I("kb"), 1.0, A.add)
+        tt(F("ov"), F("ov"), X("bfl"), A.mult)
+        ts(F("t2p"), I("t2"), 1.0, A.add)
+        ts(F("o14"), F("ov"), 16384.0, A.mult)
+        tt(F("rB"), F("kb1"), X("bfl"), A.mult)
+        tt(F("z"), F("o14"), F("t2p"), A.max)
+        ts(I("vb"), mi, 0x0F3FF8, AND)
+        tt(F("nb"), F("z"), I("t1"), A.add)
+        ts(F("vb1"), I("vb"), 65536.0, A.add)
+        tt(F("nb"), F("nb"), X("bfl"), A.mult)
+        tt(F("vB"), F("vb1"), F("ov"), A.mult)
+        if not last:
+            mm(cols("pM", 16, 32, "pM:w"), [(cols("RK", 0, 128), X("bfl"))])
+        for m0, m1 in lpieces[1 if t else 2:]:
+            lemma(m0, m1)
+        do("S", toks("DL", 0, HB), toks("AB", 0, HB),
+           [lambda: s_.activation(out=T.AB[:, 0:HB, :], in_=T.DL[:, 0:HB, :], func=AF.Abs)])
+        for kk in range(8):
+            bank = "pD%d" % (kk % 2)
+            calls = []
+            for j in range(2):
+                o = T[bank][:, HB:16, 16 * j:16 * j + 16]
+                calls.append(lambda o=o, k=2 * kk + j: p.matmul(o, T.ID[:], T.PL[:, HB:16, rows_of(t, k)], True, False))
+                calls.append(lambda o=o: p.matmul(o, T.NID[:], T.yv[:, 16 * HB:256], False, True))
+            do("P", ["ID", "NID", "yv"] + toks("PL", HB, 16), [bank], calls)
+            do("S", [bank], toks("AB%d" % kk, HB, 16),
+               [lambda kk=kk, bank=bank: s_.activation(out=T.AB[:, HB:16, 32 * kk:32 * kk + 32], in_=T[bank][:, HB:16, :], func=AF.Abs)])
+        sums(t, "AB", "pS", "SELS", "KB", 0, HB)
+        sums(1, "AB", "pS", "SELS", "KB", HB, 16, [x for kk in range(8) for x in toks("AB%d" % kk, HB, 16)])
+        if not last:
+            act(cols("RLM", c1, c1 + 256, "RLM_%d" % (t + 1)), X("RK"), AF.Copy, T.limf[:, t + 1:t + 2], extra=["limf"])
+        tt(I("uu"), F("u"), F("u"), A.mult)
+        ts(F("v37"), F("u"), 37.0, A.mult, float(t), A.add)
+        ts(I("uu"), I("uu"), 5, SHR)
+        tt(I("fs"), I("uu"), F("v37"), A.add)
+        ts(I("fs"), I("fs"), 2047, AND)
+        ts(F("new8"), I("fs"), 8.0, A.mult, 65536.0, A.add)
+        if not last:
+            cp(I("w"), cols("pM", 16, 32, "pM:w"))
+            ts(I("w"), I("w"), 3, AND)
+        keyed(X("key"), "pL", lk)
+        scan(X("SG"), X("D0"), X("key"), A.max, A.min)
+        mg = final("SG")
+        tt(F("gf"), mg, F("thr"), A.is_lt)
+        tt(F("ng"), F("sP"), mg, A.add)
+        ts(I("gi"), mg, CAP - 1, A.min)
+        tt(F("ngm"), F("ng"), F("gf"), A.mult)
+        tt(F("gs"), F("gf"), F("s1"), A.mult)
+        tt(first("EVC"), F("ngm"), F("nb"), A.max)
+        tt(first("ERC"), F("gs"), F("rB"), A.max)
+        ts(I("a"), I("gi"), 3, SHR, 2047, AND)
+        ts(F("g2"), F("gf"), -2048.0, A.mult, 2048.0, A.add)
+        update("C", "ERC", "EVC", "RC", "eC", pk, opk)
+        if not last:
+            ts(X("i1"), opk, 3, SHR, 4095, AND)
+            cp(cols("oC16", c0, c1, "oC16_%d" % t), X("i1"))
+            send("C16", t)
+            send("PK", t)
+        tt(I("al"), I("a"), F("g2"), A.max)
+        tt(F("x"), F("u32"), I("a"), A.mult)
+        cp(cols("U16", 0, 16, "a16"), I("al"))
+        ts(F("a97"), I("a"), 97.0 * t - 131072.0 - 31.0 / 64, A.add)
+        tt(I("h"), F("x"), F("a97"), A.add)
+        do("V", ["P", "Pz", "a16", "yv"], ["mn"],
+           [lambda: v.tensor_tensor(out=T.mn[:], in0=T.P[:, 0:2064].indirect(T.U16[:, 0:16]), in1=T.yv[:], op=A.min)])
+        ts(I("h"), I("h"), 1792, AND)
+        ts(F("cg"), F("g2"), 1.125, A.mult)
+        tt(F("cg"), F("cg"), X("cb"), A.add)
+        tt(F("n"), I("h"), F("cg"), A.add)
+        cp(cols("U16", 16, 32, "n16"), F("n"))
+        do("V", ["P", "Pz", "a16", "yv"], ["dv"],
+           [lambda: v.tensor_tensor(out=T.dv[:], in0=T.P[:, 0:2064].indirect(T.U16[:, 0:16]), in1=T.yv[:], op=A.subtract)])
+        do("V", ["mn", "n16"], ["P"],
+           [lambda: v.tensor_copy(out=T.P[:, 0:4352].indirect(T.U16[:, 16:32]), in_=T.mn[:])])
+        act(X("yv"), X("dv"), AF.Abs)
+        if not last:
+            mm(X("pY", (slice(None), slice(0, 16))), [(X("ID"), X("yv"))])
+            u_sum()
+        if last:
+            masks(opk, "Yp")
+            store("Y", "zp", cols("P", 0, 2048))
+            store("Y", "zy", X("yv"))
+            turn("Yp", X("i0"))
+            ts(X("i1"), X("i0"), 3, SHR, 4095, AND)
+            ts(X("i2"), X("i0"), 7, AND)
+            ts(X("f0"), X("i1"), 2048.0, A.is_ge)
+            ts(X("f2"), X("i1"), -2048.0, A.add)
+            ts(X("f0"), X("f0"), -4097.0, A.mult, 4096.0, A.add)
+            tt(X("h0"), X("f2"), X("i2"), A.max)
+            tt(X("f1"), X("i1"), X("f0"), A.min)
+            ts(X("i2"), X("i0"), 16, SHR, 15, AND)
+            store("Y", "zb", X("h0"))
+            store("Y", "zc", X("f1"))
+            cp(X("h1"), X("i2"))
+            store("Y", "zo", X("h1"))
+        do("V", whole("pS") + ["D0"], ["SC"],
+           [lambda: v.tensor_tensor_scan(out=T.SC[:], data0=T.D0[:], data1=T.pS[:, 0:256], initial=0.0, op0=A.max, op1=A.min)])
+        ts(I("gk"), I("gi"), 0x1F0000, AND)
+        cp(I("ks"), final("SC"))
+        ts(F("n8"), F("n"), 8.0, A.mult)
+        ts(I("ks"), I("ks"), 15, AND)
+        tt(F("any"), X("bfl"), F("gf"), A.max)
+        tt(F("vG"), F("n8"), I("gk"), A.add)
+        ts(F("k16"), I("ks"), 65536.0, A.mult)
+        ts(F("cf"), F("any"), -1.0, A.mult, 1.0, A.add)
+        tt(F("vG"), F("vG"), F("gf"), A.mult)
+        tt(F("vC"), F("k16"), F("new8"), A.add)
+        tt(F("vG"), F("vG"), F("vB"), A.max)
+        tt(F("vC"), F("vC"), F("cf"), A.mult)
+        tt(I("vl"), F("vG"), F("vC"), A.max)
+        ts(I("rl"), I("vl"), 16, SHR)
+        cp(first("EVL"), I("vl"))
+        cp(first("ERL"), I("rl"))
+        update("L", "ERL", "EVL", "RL", "eL", lk, olk)
+        if not last:
+            ts(X("i2"), olk, 3, SHR, 2047, AND)
+            cp(cols("oL16", c0, c1, "oL16_%d" % t), X("i2"))
+            send("L16", t)
+            send("LK", t)
+
+    masks(X("zLK"), "Yl")
+    turn("Yl", X("i0"))
+    ts(X("i1"), X("i0"), 3, SHR, 2047, AND)
+    cp(X("f3"), X("i1"))
+    store("Y", "zl", X("f3"))
+    g.sync.wait_ge(T.sem.outs, stores[0])
+    g.wait_ge(T.sem.sent, sent[0])
+    for s in cnt:
+        g.wait_ge(T.sem[s], cnt[s])

@@ -1,7 +1,7 @@
 from concourse.mybir import AluOpType as A, ActivationFunctionType as AF, AxisListType as AX
 
 TV, HOP = 6, 5
-BIG = float(2 ** 25)
+BIG = float(2 ** 26)
 CAP = float(2 ** 24)
 W = 256
 SCRATCH = {
@@ -55,7 +55,7 @@ def rank_program(g, core, T, topo):
     cnt = {}
     seen = {q: {} for q in eng}
     snap = {}
-    wrote, read = {}, {}
+    ops, wrote, read, run = [], {}, {}, {}
 
     def require(q, dep):
         s, n = dep
@@ -66,49 +66,92 @@ def rank_program(g, core, T, topo):
             if seen[q].get(a, 0) < b:
                 seen[q][a] = b
 
-    def order(q, reads, writes):
-        deps = {}
-        for t in reads + writes:
-            for s, n in wrote.get(t, []):
-                deps[s] = max(deps.get(s, 0), n)
-        for t in writes:
-            for s, n in read.get(t, {}).values():
-                deps[s] = max(deps.get(s, 0), n)
-        own = "q" + q
-        for s in sorted(deps, key=lambda s: s == own):
-            require(q, (s, deps[s]))
-
-    def note(q, reads, writes, dep):
-        snap[dep] = dict(seen[q])
-        for t in reads:
-            read.setdefault(t, {})[q] = dep
-        for t in writes:
-            wrote[t] = [dep]
-            read[t] = {}
-
     banks = {"pC", "pL", "pS", "pM", "pY", "pT", "pD0", "pD1"}
-    bank_use = {}
 
-    def do(q, reads, writes, calls):
-        order(q, reads, writes)
-        used = {t.split(":")[0] for t in reads + writes} & banks
-        for b in sorted(used):
-            for qq, dep in bank_use.get(b, {}).items():
-                if qq != q:
-                    require(q, dep)
-        s = "q" + q
-        for c in calls:
-            c().then_inc(T.sem[s], 1)
-            cnt[s] = cnt.get(s, 0) + 1
-        note(q, reads, writes, (s, cnt[s]))
-        for b in used:
-            bank_use.setdefault(b, {})[q] = (s, cnt[s])
+    def do(q, reads, writes, calls, us=0.06, kind="call"):
+        i, deps = len(ops), set()
+        for t in reads + writes:
+            deps |= wrote.get(t, set())
+        for t in writes:
+            deps |= read.get(t, set())
+        for b in {t.split(":")[0] for t in reads + writes} & banks:
+            r = run.setdefault(b, [q, [], []])
+            if r[0] != q:
+                run[b] = r = [q, [], r[1]]
+            r[1].append(i)
+            deps |= set(r[2])
+        for t in writes:
+            wrote[t], read[t] = {i}, set()
+        for t in reads:
+            read.setdefault(t, set()).add(i)
+        deps.discard(i)
+        ops.append({"q": q, "deps": deps, "calls": calls, "us": us, "kind": kind})
+        return ops[-1]
 
-    def X(name, idx=None, tok=None):
-        return (T[name][:] if idx is None else T[name][idx], tok or name)
+    def emit():
+        lat, slack = 0.12, 0.1
+        n = len(ops)
+        succ, left = [[] for _ in ops], [len(o["deps"]) for o in ops]
+        for i, o in enumerate(ops):
+            for d in o["deps"]:
+                succ[d].append(i)
+        prio, start, end, rdy = [0.0] * n, [0.0] * n, [0.0] * n, [0.0] * n
+        for i in range(n - 1, -1, -1):
+            prio[i] = -i
+        free, pool = {q: 0.0 for q in "VSPGYN"}, {q: set() for q in "VSPGYN"}
+        for i in range(n):
+            if not left[i]:
+                pool[ops[i]["q"]].add(i)
+        done = []
+        while len(done) < n:
+            best = None
+            for q, c in pool.items():
+                if not c:
+                    continue
+                f = free[q] if q != "N" else 0.0
+                top = max(c, key=lambda i: (prio[i], -i))
+                lim = max(f, rdy[top]) + slack
+                fit = [i for i in c if q == "V" and i < top + 30 and max(f, rdy[i]) + ops[i]["us"] <= lim]
+                pick = min(fit, key=lambda i: (max(f, rdy[i]), -prio[i], i)) if fit and rdy[top] > f else top
+                s = max(f, rdy[pick])
+                if best is None or s < best[0]:
+                    best = (s, q, pick)
+            s, q, i = best
+            pool[q].discard(i)
+            start[i], end[i] = s, s + ops[i]["us"]
+            free[q] = end[i]
+            done.append(i)
+            for j in succ[i]:
+                left[j] -= 1
+                rdy[j] = max(rdy[j], end[i] + lat)
+                if not left[j]:
+                    pool[ops[j]["q"]].add(j)
+        for i in done:
+            o = ops[i]
+            q = o["q"]
+            if o["kind"] == "land":
+                continue
+            deps = {}
+            for d in o["deps"]:
+                a, b = ops[d]["sig"]
+                deps[a] = max(deps.get(a, 0), b)
+            for a in sorted(deps, key=lambda a: a == "q" + q):
+                require(q, (a, deps[a]))
+            if o["kind"] == "call":
+                a = "q" + q
+                for c in o["calls"]:
+                    c().then_inc(T.sem[a], 1)
+                    cnt[a] = cnt.get(a, 0) + 1
+                o["sig"] = (a, cnt[a])
+                snap[o["sig"]] = dict(seen[q])
+            else:
+                o["calls"]()
+
+    def X(name, idx=None, tok=None, n=256):
+        return (T[name][:] if idx is None else T[name][idx], tok or name, n)
 
     def cols(name, a, b, tok=None):
-        return X(name, (slice(None), slice(a, b)), tok)
+        return X(name, (slice(None), slice(a, b)), tok, b - a)
 
     lanes = {"LF": {}, "LI": {}}
 
@@ -123,45 +166,52 @@ def rank_program(g, core, T, topo):
         return lane("LI", n)
 
     def first(name):
-        return X(name, (slice(None), slice(0, 256, 16)))
+        return X(name, (slice(None), slice(0, 256, 16)), None, 16)
 
     def final(name):
-        return X(name, (slice(None), slice(15, 256, 16)))
+        return X(name, (slice(None), slice(15, 256, 16)), None, 16)
+
+    def cyc(n):
+        return max(64, n) * 0.83e-3
 
     v, s_, p = g.vector, g.scalar, g.tensor
 
     def tt(o, a, b, op):
-        do("V", [a[1], b[1]], [o[1]], [lambda: v.tensor_tensor(out=o[0], in0=a[0], in1=b[0], op=op)])
+        do("V", [a[1], b[1]], [o[1]], [lambda: v.tensor_tensor(out=o[0], in0=a[0], in1=b[0], op=op)],
+           cyc(o[2] * (1 if {a[1].split(":")[0], b[1].split(":")[0]} & banks else 2)))
 
     def ts(o, a, s1, op0, s2=None, op1=None, extra=()):
         kw = {"op1": op1} if op1 is not None else {}
         do("V", [a[1]] + list(extra), [o[1]],
-           [lambda: v.tensor_scalar(out=o[0], in0=a[0], scalar1=s1, scalar2=s2, op0=op0, **kw)])
+           [lambda: v.tensor_scalar(out=o[0], in0=a[0], scalar1=s1, scalar2=s2, op0=op0, **kw)], cyc(o[2]))
 
     def cp(o, a):
-        do("V", [a[1]], [o[1]], [lambda: v.tensor_copy(out=o[0], in_=a[0])])
+        do("V", [a[1]], [o[1]], [lambda: v.tensor_copy(out=o[0], in_=a[0])], cyc(o[2]))
 
     def fill(o, c):
-        do("V", [], [o[1]], [lambda: v.memset(o[0], c)])
+        do("V", [], [o[1]], [lambda: v.memset(o[0], c)], 0.2 if o[1] != "SELC" else 0.9)
 
     def scan(o, d0, d1, op0, op1):
-        do("V", [d0[1], d1[1]], [o[1]], [lambda: v.tensor_tensor_scan(out=o[0], data0=d0[0], data1=d1[0], initial=0.0, op0=op0, op1=op1)])
+        do("V", [d0[1], d1[1]], [o[1]],
+           [lambda: v.tensor_tensor_scan(out=o[0], data0=d0[0], data1=d1[0], initial=0.0, op0=op0, op1=op1)], cyc(o[2]))
 
-    def act(o, a, func, scale=1.0, extra=()):
-        do("S", [a[1]] + list(extra), [o[1]], [lambda: s_.activation(out=o[0], in_=a[0], func=func, scale=scale)])
+    def act(o, a, func, scale=1.0, bias=0.0, extra=()):
+        do("S", [a[1]] + list(extra), [o[1]], [lambda: s_.activation(out=o[0], in_=a[0], func=func, scale=scale, bias=bias)],
+           cyc(o[2]) if o[1] != "SELS" else 1.7)
 
     def mm(o, pairs):
         reads = [t[1] for pr in pairs for t in pr]
         n = len(pairs)
-        do("P", reads, [o[1]], [(lambda i=i, l=l, r=r: p.matmul(o[0], l[0], r[0], i == 0, i == n - 1)) for i, (l, r) in enumerate(pairs)])
+        do("P", reads, [o[1]], [(lambda i=i, l=l, r=r: p.matmul(o[0], l[0], r[0], i == 0, i == n - 1)) for i, (l, r) in enumerate(pairs)],
+           n * max(64, o[2]) * 0.42e-3)
 
     SHR, AND = A.logical_shift_right, A.bitwise_and
 
     def load(q, name, dst):
         s = "ld_" + name
-        eng[q].dma_start(dst[0], T[name][:]).then_inc(T.sem[s], 16)
         cnt[s] = 16
-        note(q, [], [dst[1]], (s, 16))
+        eng[q].dma_start(dst[0], T[name][:]).then_inc(T.sem[s], 16)
+        do("N", [], [dst[1]], [], 4.5 if name == "prop" else 2.3, "land")["sig"] = (s, 16)
     load("Y", "con", X("conA"))
     load("S", "prop", cols("P", 0, 2048))
     load("Y", "ex", X("yv"))
@@ -171,10 +221,10 @@ def rank_program(g, core, T, topo):
     load("Y", "lim", X("limA"))
 
     def sel(o, a, pat, cmp, fillv, base, cm):
-        do("G", [a[1]], [o[1]], [lambda: g.affine_select(o[0], a[0], pat, cmp, fillv, base, cm)])
+        do("G", [a[1]], [o[1]], [lambda: g.affine_select(o[0], a[0], pat, cmp, fillv, base, cm)], 0.17 + 2 * cyc(o[2]))
 
     def iota(o, pat, base, cm):
-        do("G", [], [o[1]], [lambda: g.iota(o[0], pat, base, cm, allow_small_or_imprecise_dtypes=True)])
+        do("G", [], [o[1]], [lambda: g.iota(o[0], pat, base, cm, allow_small_or_imprecise_dtypes=True)], 0.13 + 2 * cyc(o[2]))
     fill(X("ones"), 1.0)
     one128 = cols("ones", 0, 128)
     sel(X("ID"), one128, [[-1, 128]], A.is_equal, 0.0, 0, 1)
@@ -197,9 +247,9 @@ def rank_program(g, core, T, topo):
     cp(cols("C16", 0, 256, "C16_0"), X("f1"))
     mm(X("pY", (slice(None), slice(0, 16))), [(X("ID"), X("yv"))])
     cp(cols("L16", 0, 256, "L16_0"), X("lemA"))
-    for i in range(16):
-        b8 = X("BLK", (slice(None), slice(0, 128, 16)))
-        ts(X("SELC", (slice(None), slice(129 * i, 128 * i + 128, 16))), b8, -BIG, A.mult)
+    do("V", ["BLK"], ["SELC"],
+       [(lambda i=i: v.tensor_scalar(out=T.SELC[:, 129 * i:128 * i + 128:16], in0=T.BLK[:, 0:128:16], scalar1=-BIG, scalar2=None,
+                                     op0=A.mult)) for i in range(16)], 0.9)
 
     def selq(nm, q):
         return cols(nm, 128 * q, 128 * q + 128, nm)
@@ -210,7 +260,7 @@ def rank_program(g, core, T, topo):
         win = T.P[:, 0:2064].indirect(T[lst][:, 256 * t + 16 * m:256 * t + 16 * m + 16])
         out = T[dst][:, m, :]
         do(q, [tok, "P", "Pz"], ["%s:%d" % (dst, m)],
-           [(lambda: s_.activation(out=out, in_=win, func=AF.Copy)) if q == "S" else (lambda: v.tensor_copy(out=out, in_=win))])
+           [(lambda: s_.activation(out=out, in_=win, func=AF.Copy)) if q == "S" else (lambda: v.tensor_copy(out=out, in_=win))], 0.39)
 
     def rows_of(t, k):
         return slice(k, 256, 16) if t == 0 else slice(16 * k, 16 * k + 16)
@@ -225,20 +275,21 @@ def rank_program(g, core, T, topo):
         ms = slice(m0, m1)
         do("V", toks(src, m0, m1) + ["pY"], toks(dst, m0, m1),
            [(lambda k=k: v.tensor_tensor(out=T[dst][:, ms, rows_of(t, k)], in0=T[src][:, ms, rows_of(t, k)], in1=T.pY[:, ms, :], op=op))
-            for k in range(16)])
+            for k in range(16)], 16 * cyc(16 * (m1 - m0)))
 
     def sums(t, src, bank, sl, const, m0, m1, made=None):
         ms, cs = slice(m0, m1), slice(16 * m0, 16 * m1)
         out = T[bank][:, cs]
         calls = [lambda: p.matmul(out, T.ID[:], T[const][:, cs], True, False)]
         calls += [(lambda q=q: p.matmul(out, T[sl][:, 128 * q:128 * q + 128], T[src][:, ms, lanes_of(t, q)], False, q == 15)) for q in range(16)]
-        do("P", ["ID", const, sl] + (made or toks(src, m0, m1)), ["%s:%d" % (bank, m) for m in range(m0, m1)], calls)
+        do("P", ["ID", const, sl] + (made or toks(src, m0, m1)), ["%s:%d" % (bank, m) for m in range(m0, m1)], calls,
+           17 * max(64, 16 * (m1 - m0)) * 0.42e-3)
 
     def whole(bank):
         return [("%s:%d" % (bank, m)) for m in range(16)]
 
     def keyed(o, bank, b):
-        do("V", whole(bank) + [b[1]], [o[1]], [lambda: v.tensor_tensor(out=o[0], in0=T[bank][:, 0:256], in1=b[0], op=A.max)])
+        do("V", whole(bank) + [b[1]], [o[1]], [lambda: v.tensor_tensor(out=o[0], in0=T[bank][:, 0:256], in1=b[0], op=A.max)], cyc(256))
 
     cpieces = [(0, 8), (8, 16)]
     HB = 4
@@ -253,8 +304,10 @@ def rank_program(g, core, T, topo):
     def send(kind, t):
         c = slice(256 * t, 256 * t + 256)
         d = slice(256 * t + 256, 256 * t + 512)
-        order("G", ["o%s_%d" % (kind, t)], [])
-        g.remote_dma(T[kind][:, d], T["o" + kind][:, c], T.sem["a%s_%d" % (kind, t + 1)], T.sem.sent, pid, rid, msk)
+        a = "a%s_%d" % (kind, t + 1)
+        do("G", ["o%s_%d" % (kind, t)], ["net" + a],
+           lambda: g.remote_dma(T[kind][:, d], T["o" + kind][:, c], T.sem[a], T.sem.sent, pid, rid, msk), 0.8, "send")
+        do("N", ["net" + a], ["%s_%d" % (kind, t + 1)], [], 3.0, "land")["sig"] = (a, neng)
         sent[0] += neng
 
     def masks(src, y):
@@ -262,7 +315,7 @@ def rank_program(g, core, T, topo):
             act(X(y, (slice(None), slice(None), slice(16 * e, 16 * e + 16)), "%s%d" % (y, e)), src, AF.Copy, T.col[:, e:e + 1], extra=["col"])
 
     def turn(y, dst):
-        do("V", [y + "0", y + "1"], ["Z"], [(lambda m=m: v.transpose(out=T.Z[:, m, :], in_=T[y][:, m, :])) for m in range(16)])
+        do("V", [y + "0", y + "1"], ["Z"], [(lambda m=m: v.transpose(out=T.Z[:, m, :], in_=T[y][:, m, :])) for m in range(16)], 0.85)
         tt(dst, X("Z", (slice(None), slice(None), slice(0, 16))), X("Z", (slice(None), slice(None), slice(16, 32))), A.add)
 
     def consts():
@@ -298,16 +351,17 @@ def rank_program(g, core, T, topo):
     sel(X("D0"), X("fb"), [[0, 16], [1, 16]], A.is_gt, float(2 ** 30), 0, 0)
     sel(X("D1"), X("SC"), [[0, 16], [1, 16]], A.is_gt, 0.0, 0, 0)
 
-    def u_sum():
+    def u_sum(t):
         mm(cols("pM", 0, 16, "pM:u"), [(selq("SELS", q), yr[q]) for q in range(16)])
         act(F("u"), cols("pM", 0, 16, "pM:u"), AF.Copy, 1.0 / 16)
-        act(F("u32"), cols("pM", 0, 16, "pM:u"), AF.Copy, 1.0 / 512)
+        act(F("u32"), cols("pM", 0, 16, "pM:u"), AF.Identity, 1.0 / 512, 1.0)
+        act(F("v37"), cols("pM", 0, 16, "pM:u"), AF.Identity, 37.0 / 16, float(t))
 
-    def update(tag, e_row, e_val, R, e, old, new):
+    def update(e_row, e_val, R, e, at, old, new):
         pa, pb = cols("pT", 0, 256, "pT:a"), cols("pT", 256, 512, "pT:b")
         scan(X(R), X("D1h"), X(e_row), A.mult, A.add)
         scan(pa, X("D1"), X(e_val), A.mult, A.add)
-        ts(X(e), X(R), 1.0, A.is_equal)
+        ts(X(e), X(R), at, A.is_equal)
         tt(pb, pa, old, A.subtract)
         tt(pa, pb, X(e), A.mult)
         tt(new, pa, old, A.add)
@@ -315,8 +369,7 @@ def rank_program(g, core, T, topo):
     stores = [0]
 
     def store(q, name, src):
-        order(q, [src[1]], [])
-        eng[q].dma_start(T[name][:], src[0]).then_inc(T.sem.outs, 16)
+        do(q, [src[1]], [], lambda: eng[q].dma_start(T[name][:], src[0]).then_inc(T.sem.outs, 16), 0.1, "store")
         stores[0] += 16
 
     for t in range(TV):
@@ -326,10 +379,6 @@ def rank_program(g, core, T, topo):
         opk, olk = cols("oPK", c0, c1, "oPK_%d" % t), cols("oLK", c0, c1, "oLK_%d" % t)
         if last:
             opk, olk = X("zPK"), X("zLK")
-        if t:
-            for k in _KINDS:
-                dep = ("a%s_%d" % (k, t), neng)
-                wrote["%s_%d" % (k, t)] = [dep]
         if t == 0:
             consts()
             ts(cols("RLM", 0, 256, "RLM_0"), X("RK"), T.limf[:, 0:1], A.mult, extra=["limf"])
@@ -343,7 +392,8 @@ def rank_program(g, core, T, topo):
             if m0 < HB:
                 compare(t, "PL", "DL", A.subtract, m0, m1)
                 do("V", toks("DL", m0, m1), toks("XL", m0, m1),
-                   [lambda: v.tensor_scalar(out=T.XL[:, m0:m1, :], in0=T.DL[:, m0:m1, :], scalar1=0.0, scalar2=None, op0=A.is_gt)])
+                   [lambda: v.tensor_scalar(out=T.XL[:, m0:m1, :], in0=T.DL[:, m0:m1, :], scalar1=0.0, scalar2=None, op0=A.is_gt)],
+                   cyc(128 * (m1 - m0)))
             else:
                 compare(t, "PL", "XL", A.is_gt, m0, m1)
             sums(t, "XL", "pL", "SELC", "THR", m0, m1)
@@ -362,7 +412,7 @@ def rank_program(g, core, T, topo):
             lemma(*lpieces[0])
             turn("Yl", cols("LK", 0, 256, "LK_0"))
             lemma(*lpieces[1])
-            u_sum()
+            u_sum(0)
         lp = cols("pM", 256, 512, "pM:l")
         mm(lp, [(X("BLK"), cols("RLM", c0, c1, "RLM_%d" % t))])
         x, sl = X("i0"), I("sl")
@@ -373,7 +423,6 @@ def rank_program(g, core, T, topo):
         ts(sl, final("SS"), 16.0, A.mult)
         ts(sl, sl, 15, AND)
         ts(F("sP"), sl, float(2 ** 20), A.mult, -65536.0, A.add)
-        ts(F("s1"), sl, 1.0, A.add)
         if t:
             for m0, m1 in cpieces:
                 conditions(m0, m1)
@@ -382,48 +431,43 @@ def rank_program(g, core, T, topo):
         scan(X("SB"), X("D0"), X("key"), A.max, A.min)
         mb, mi = final("SB"), I("mi")
         ts(X("bfl"), mb, CAP, A.is_lt)
-        ts(mi, mb, CAP - 1, A.min)
-        ts(F("thr"), X("bfl"), -CAP, A.mult, CAP, A.add)
+        ts(mi, mb, CAP + 49152.0, A.min)
         ts(I("lim"), mi, 14, SHR, 3, AND)
         ts(I("b"), mi, 7, AND)
-        ts(I("kb"), mi, 20, SHR)
         ts(I("t2"), mi, 0x3FFF, AND)
+        ts(I("t1"), mi, 0x1FF0000, AND)
         tt(F("bl"), I("b"), I("lim"), A.subtract)
-        ts(I("t1"), mi, 0xFF0000, AND)
-        tt(F("ov"), F("bl"), I("w"), A.is_ge)
-        ts(F("kb1"), I("kb"), 1.0, A.add)
-        tt(F("ov"), F("ov"), X("bfl"), A.mult)
         ts(F("t2p"), I("t2"), 1.0, A.add)
-        ts(F("o14"), F("ov"), 16384.0, A.mult)
-        tt(F("rB"), F("kb1"), X("bfl"), A.mult)
-        tt(F("z"), F("o14"), F("t2p"), A.max)
         ts(I("vb"), mi, 0x0F3FF8, AND)
-        tt(F("nb"), F("z"), I("t1"), A.add)
+        tt(F("ov"), F("bl"), I("w"), A.is_ge)
         ts(F("vb1"), I("vb"), 65536.0, A.add)
-        tt(F("nb"), F("nb"), X("bfl"), A.mult)
+        ts(F("tb"), mb, CAP, A.is_lt, 2 * CAP, A.mult)
+        ts(F("o14"), F("ov"), 16384.0, A.mult)
         tt(F("vB"), F("vb1"), F("ov"), A.mult)
+        tt(F("z"), F("o14"), F("t2p"), A.max)
+        tt(F("nb"), F("z"), I("t1"), A.add)
         if not last:
             mm(cols("pM", 16, 32, "pM:w"), [(cols("RK", 0, 128), X("bfl"))])
         for m0, m1 in lpieces[1 if t else 2:]:
             lemma(m0, m1)
         do("S", toks("DL", 0, HB), toks("AB", 0, HB),
-           [lambda: s_.activation(out=T.AB[:, 0:HB, :], in_=T.DL[:, 0:HB, :], func=AF.Abs)])
+           [lambda: s_.activation(out=T.AB[:, 0:HB, :], in_=T.DL[:, 0:HB, :], func=AF.Abs)], cyc(256 * HB))
         for kk in range(8):
             bank = "pD%d" % (kk % 2)
             calls = []
             for j in range(2):
                 o = T[bank][:, HB:16, 16 * j:16 * j + 16]
-                calls.append(lambda o=o, k=2 * kk + j: p.matmul(o, T.ID[:], T.PL[:, HB:16, rows_of(t, k)], True, False))
+                calls.append(lambda o=o, r=rows_of(t, 2 * kk + j): p.matmul(o, T.ID[:], T.PL[:, HB:16, r], True, False))
                 calls.append(lambda o=o: p.matmul(o, T.NID[:], T.yv[:, 16 * HB:256], False, True))
-            do("P", ["ID", "NID", "yv"] + toks("PL", HB, 16), [bank], calls)
+            do("P", ["ID", "NID", "yv"] + toks("PL", HB, 16), [bank], calls, 4 * 16 * (16 - HB) * 0.42e-3)
             do("S", [bank], toks("AB%d" % kk, HB, 16),
-               [lambda kk=kk, bank=bank: s_.activation(out=T.AB[:, HB:16, 32 * kk:32 * kk + 32], in_=T[bank][:, HB:16, :], func=AF.Abs)])
+               [lambda kk=kk, bank=bank: s_.activation(out=T.AB[:, HB:16, 32 * kk:32 * kk + 32], in_=T[bank][:, HB:16, :], func=AF.Abs)],
+               cyc(32 * (16 - HB)))
         sums(t, "AB", "pS", "SELS", "KB", 0, HB)
         sums(1, "AB", "pS", "SELS", "KB", HB, 16, [x for kk in range(8) for x in toks("AB%d" % kk, HB, 16)])
         if not last:
             act(cols("RLM", c1, c1 + 256, "RLM_%d" % (t + 1)), X("RK"), AF.Copy, T.limf[:, t + 1:t + 2], extra=["limf"])
         tt(I("uu"), F("u"), F("u"), A.mult)
-        ts(F("v37"), F("u"), 37.0, A.mult, float(t), A.add)
         ts(I("uu"), I("uu"), 5, SHR)
         tt(I("fs"), I("uu"), F("v37"), A.add)
         ts(I("fs"), I("fs"), 2047, AND)
@@ -434,41 +478,38 @@ def rank_program(g, core, T, topo):
         keyed(X("key"), "pL", lk)
         scan(X("SG"), X("D0"), X("key"), A.max, A.min)
         mg = final("SG")
-        tt(F("gf"), mg, F("thr"), A.is_lt)
         tt(F("ng"), F("sP"), mg, A.add)
-        ts(I("gi"), mg, CAP - 1, A.min)
-        tt(F("ngm"), F("ng"), F("gf"), A.mult)
-        tt(F("gs"), F("gf"), F("s1"), A.mult)
-        tt(first("EVC"), F("ngm"), F("nb"), A.max)
-        tt(first("ERC"), F("gs"), F("rB"), A.max)
-        ts(I("a"), I("gi"), 3, SHR, 2047, AND)
-        ts(F("g2"), F("gf"), -2048.0, A.mult, 2048.0, A.add)
-        update("C", "ERC", "EVC", "RC", "eC", pk, opk)
+        tt(F("q"), F("ng"), F("tb"), A.max)
+        tt(I("vc"), F("q"), F("nb"), A.min)
+        ts(I("gq"), F("q"), CAP + 16384.0, A.min)
+        ts(I("kc"), I("vc"), 20, SHR)
+        cp(first("EVC"), I("vc"))
+        cp(first("ERC"), I("kc"))
+        ts(I("al"), I("gq"), 3, SHR, 4095, AND)
+        update("ERC", "EVC", "RC", "eC", 0.0, pk, opk)
         if not last:
             ts(X("i1"), opk, 3, SHR, 4095, AND)
             cp(cols("oC16", c0, c1, "oC16_%d" % t), X("i1"))
             send("C16", t)
             send("PK", t)
-        tt(I("al"), I("a"), F("g2"), A.max)
-        tt(F("x"), F("u32"), I("a"), A.mult)
         cp(cols("U16", 0, 16, "a16"), I("al"))
-        ts(F("a97"), I("a"), 97.0 * t - 131072.0 - 31.0 / 64, A.add)
-        tt(I("h"), F("x"), F("a97"), A.add)
+        tt(F("x"), F("u32"), I("al"), A.mult)
+        ts(F("cg"), I("al"), 2048.0, A.is_ge, 2304.0, A.mult)
+        ts(I("h"), F("x"), 97.0 * t - 131072.0 - 31.0 / 64, A.add)
         do("V", ["P", "Pz", "a16", "yv"], ["mn"],
-           [lambda: v.tensor_tensor(out=T.mn[:], in0=T.P[:, 0:2064].indirect(T.U16[:, 0:16]), in1=T.yv[:], op=A.min)])
+           [lambda: v.tensor_tensor(out=T.mn[:], in0=T.P[:, 0:2064].indirect(T.U16[:, 0:16]), in1=T.yv[:], op=A.min)], 0.4)
         ts(I("h"), I("h"), 1792, AND)
-        ts(F("cg"), F("g2"), 1.125, A.mult)
         tt(F("cg"), F("cg"), X("cb"), A.add)
         tt(F("n"), I("h"), F("cg"), A.add)
         cp(cols("U16", 16, 32, "n16"), F("n"))
         do("V", ["P", "Pz", "a16", "yv"], ["dv"],
-           [lambda: v.tensor_tensor(out=T.dv[:], in0=T.P[:, 0:2064].indirect(T.U16[:, 0:16]), in1=T.yv[:], op=A.subtract)])
+           [lambda: v.tensor_tensor(out=T.dv[:], in0=T.P[:, 0:2064].indirect(T.U16[:, 0:16]), in1=T.yv[:], op=A.subtract)], 0.4)
         do("V", ["mn", "n16"], ["P"],
-           [lambda: v.tensor_copy(out=T.P[:, 0:4352].indirect(T.U16[:, 16:32]), in_=T.mn[:])])
+           [lambda: v.tensor_copy(out=T.P[:, 0:4352].indirect(T.U16[:, 16:32]), in_=T.mn[:])], 0.7)
         act(X("yv"), X("dv"), AF.Abs)
         if not last:
             mm(X("pY", (slice(None), slice(0, 16))), [(X("ID"), X("yv"))])
-            u_sum()
+            u_sum(t + 1)
         if last:
             masks(opk, "Yp")
             store("Y", "zp", cols("P", 0, 2048))
@@ -487,15 +528,15 @@ def rank_program(g, core, T, topo):
             cp(X("h1"), X("i2"))
             store("Y", "zo", X("h1"))
         do("V", whole("pS") + ["D0"], ["SC"],
-           [lambda: v.tensor_tensor_scan(out=T.SC[:], data0=T.D0[:], data1=T.pS[:, 0:256], initial=0.0, op0=A.max, op1=A.min)])
-        ts(I("gk"), I("gi"), 0x1F0000, AND)
+           [lambda: v.tensor_tensor_scan(out=T.SC[:], data0=T.D0[:], data1=T.pS[:, 0:256], initial=0.0, op0=A.max, op1=A.min)], cyc(256))
         cp(I("ks"), final("SC"))
-        ts(F("n8"), F("n"), 8.0, A.mult)
+        ts(I("gk"), I("gq"), 0x0F0000, AND)
+        ts(F("n8"), F("n"), 8.0, A.mult, 65536.0, A.add)
         ts(I("ks"), I("ks"), 15, AND)
-        tt(F("any"), X("bfl"), F("gf"), A.max)
+        ts(F("gf"), F("q"), CAP, A.is_lt)
         tt(F("vG"), F("n8"), I("gk"), A.add)
         ts(F("k16"), I("ks"), 65536.0, A.mult)
-        ts(F("cf"), F("any"), -1.0, A.mult, 1.0, A.add)
+        ts(F("cf"), I("vc"), CAP, A.is_ge)
         tt(F("vG"), F("vG"), F("gf"), A.mult)
         tt(F("vC"), F("k16"), F("new8"), A.add)
         tt(F("vG"), F("vG"), F("vB"), A.max)
@@ -504,7 +545,7 @@ def rank_program(g, core, T, topo):
         ts(I("rl"), I("vl"), 16, SHR)
         cp(first("EVL"), I("vl"))
         cp(first("ERL"), I("rl"))
-        update("L", "ERL", "EVL", "RL", "eL", lk, olk)
+        update("ERL", "EVL", "RL", "eL", 1.0, lk, olk)
         if not last:
             ts(X("i2"), olk, 3, SHR, 2047, AND)
             cp(cols("oL16", c0, c1, "oL16_%d" % t), X("i2"))
@@ -516,6 +557,7 @@ def rank_program(g, core, T, topo):
     ts(X("i1"), X("i0"), 3, SHR, 2047, AND)
     cp(X("f3"), X("i1"))
     store("Y", "zl", X("f3"))
+    emit()
     g.sync.wait_ge(T.sem.outs, stores[0])
     g.wait_ge(T.sem.sent, sent[0])
     for s in cnt:

from concourse.mybir import AluOpType as A, ActivationFunctionType as AF, AxisListType as AX

TV, HOP = 6, 5
BIG = float(2 ** 26)
CAP = float(2 ** 24)
W = 256
SCRATCH = {
    "P": ("sbuf", [128, 4352], "bfloat16"), "NID": ("sbuf", [128, 128], "bfloat16"),
    "PC": ("sbuf", [128, 16, 256], "bfloat16"), "PL": ("sbuf", [128, 16, 256], "bfloat16"),
    "XC": ("sbuf", [128, 16, 256], "bfloat16"), "XL": ("sbuf", [128, 16, 256], "bfloat16"),
    "DL": ("sbuf", [128, 16, 256], "bfloat16"), "AB": ("sbuf", [128, 16, 256], "bfloat16"),
    "yv": ("sbuf", [128, 256], "bfloat16"), "dv": ("sbuf", [128, 256], "bfloat16"), "mn": ("sbuf", [128, 256], "bfloat16"),
    "C16": ("sbuf", [128, 256 * TV], "uint16"), "L16": ("sbuf", [128, 256 * TV], "uint16"),
    "PK": ("sbuf", [128, 256 * TV], "int32"), "LK": ("sbuf", [128, 256 * TV], "int32"),
    "oC16": ("sbuf", [128, 256 * TV], "uint16"), "oL16": ("sbuf", [128, 256 * TV], "uint16"),
    "oPK": ("sbuf", [128, 256 * TV], "int32"), "oLK": ("sbuf", [128, 256 * TV], "int32"),
    "lemA": ("sbuf", [128, 256], "int32"), "conA": ("sbuf", [128, 256], "int32"), "limA": ("sbuf", [128, TV], "int32"),
    "orgA": ("sbuf", [128, 256], "bfloat16"), "cntA": ("sbuf", [128, 256], "bfloat16"),
    "f0": ("sbuf", [128, 256], "float32"), "f1": ("sbuf", [128, 256], "float32"), "f2": ("sbuf", [128, 256], "float32"),
    "f3": ("sbuf", [128, 256], "float32"), "f4": ("sbuf", [128, 256], "float32"), "zPK": ("sbuf", [128, 256], "float32"), "zLK": ("sbuf", [128, 256], "float32"),
    "i0": ("sbuf", [128, 256], "int32"), "i1": ("sbuf", [128, 256], "int32"),
    "i2": ("sbuf", [128, 256], "int32"), "h0": ("sbuf", [128, 256], "bfloat16"), "h1": ("sbuf", [128, 256], "bfloat16"),
    "KC": ("sbuf", [128, 256], "float32"), "key": ("sbuf", [128, 256], "float32"),
    "keyS": ("sbuf", [128, 256], "float32"), "SS": ("sbuf", [128, 256], "float32"),
    "SB": ("sbuf", [128, 256], "float32"), "SG": ("sbuf", [128, 256], "float32"), "SC": ("sbuf", [128, 256], "float32"),
    "RC": ("sbuf", [128, 256], "bfloat16"), "RL": ("sbuf", [128, 256], "bfloat16"),
    "eC": ("sbuf", [128, 256], "bfloat16"), "eL": ("sbuf", [128, 256], "bfloat16"),
    "EVC": ("sbuf", [128, 256], "float32"), "EVL": ("sbuf", [128, 256], "float32"),
    "ERC": ("sbuf", [128, 256], "bfloat16"), "ERL": ("sbuf", [128, 256], "bfloat16"),
    "Yp": ("sbuf", [128, 16, 32], "float32"), "Yl": ("sbuf", [128, 16, 32], "float32"), "Z": ("sbuf", [128, 16, 32], "float32"),
    "ones": ("sbuf", [128, 256], "bfloat16"), "ID": ("sbuf", [128, 128], "bfloat16"), "BT": ("sbuf", [128, 128], "bfloat16"),
    "BLK": ("sbuf", [128, 128], "bfloat16"), "RK": ("sbuf", [128, 256], "bfloat16"), "mt": ("sbuf", [128, 128], "bfloat16"),
    "SELC": ("sbuf", [128, 2048], "bfloat16"), "SELS": ("sbuf", [128, 2048], "bfloat16"),
    "THR": ("sbuf", [128, 256], "bfloat16"), "KI": ("sbuf", [128, 256], "float32"), "KB": ("sbuf", [128, 256], "bfloat16"),
    "D0": ("sbuf", [128, 256], "float32"), "D1": ("sbuf", [128, 256], "float32"), "D1h": ("sbuf", [128, 256], "bfloat16"),
    "fb": ("sbuf", [128, 256], "float32"), "RLM": ("sbuf", [128, 256 * TV], "bfloat16"), "limf": ("sbuf", [128, TV], "float32"),
    "col": ("sbuf", [128, 8], "float32"), "cb": ("sbuf", [128, 16], "float32"), "kq": ("sbuf", [128, 16], "float32"),
    "LF": ("sbuf", [128, 16 * 64], "float32"), "LI": ("sbuf", [128, 16 * 64], "int32"), "bfl": ("sbuf", [128, 16], "bfloat16"),
    "U16": ("sbuf", [128, 32], "uint16"),
    "pC": ("psum", [128, 512], "float32"), "pL": ("psum", [128, 512], "float32"), "pS": ("psum", [128, 512], "float32"),
    "pM": ("psum", [128, 512], "float32"), "pY": ("psum", [128, 32, 16], "float32"), "pT": ("psum", [128, 512], "float32"),
    "pD0": ("psum", [128, 16, 32], "float32"), "pD1": ("psum", [128, 16, 32], "float32"),
}
_LOADS = ["prop", "lem", "con", "ex", "lim", "org", "cnt"]
_KINDS = ["C16", "PK", "L16", "LK"]
SEMAPHORES = (["qV", "qS", "qP", "qG", "sent", "outs"] + ["ld_" + n for n in _LOADS]
              + ["a%s_%d" % (k, t) for k in _KINDS for t in range(1, TV)])


def rank_program(g, core, T, topo):
    rank = T.rank_of(core)
    if rank is None:
        return
    eng = {"V": g.vector, "S": g.scalar, "P": g.tensor, "G": g, "Y": g.sync}
    cnt = {}
    seen = {q: {} for q in eng}
    snap = {}
    ops, wrote, read, run = [], {}, {}, {}

    def require(q, dep):
        s, n = dep
        if seen[q].get(s, 0) >= n:
            return
        eng[q].wait_ge(T.sem[s], n)
        for a, b in list(snap.get(dep, {}).items()) + [dep]:
            if seen[q].get(a, 0) < b:
                seen[q][a] = b

    banks = {"pC", "pL", "pS", "pM", "pY", "pT", "pD0", "pD1"}

    def do(q, reads, writes, calls, us=0.06, kind="call"):
        i, deps = len(ops), set()
        for t in reads + writes:
            deps |= wrote.get(t, set())
        for t in writes:
            deps |= read.get(t, set())
        for b in {t.split(":")[0] for t in reads + writes} & banks:
            r = run.setdefault(b, [q, [], []])
            if r[0] != q:
                run[b] = r = [q, [], r[1]]
            r[1].append(i)
            deps |= set(r[2])
        for t in writes:
            wrote[t], read[t] = {i}, set()
        for t in reads:
            read.setdefault(t, set()).add(i)
        deps.discard(i)
        ops.append({"q": q, "deps": deps, "calls": calls, "us": us, "kind": kind})
        return ops[-1]

    def emit():
        lat, slack = 0.12, 0.1
        n = len(ops)
        succ, left = [[] for _ in ops], [len(o["deps"]) for o in ops]
        for i, o in enumerate(ops):
            for d in o["deps"]:
                succ[d].append(i)
        prio, start, end, rdy = [0.0] * n, [0.0] * n, [0.0] * n, [0.0] * n
        for i in range(n - 1, -1, -1):
            prio[i] = -i
        free, pool = {q: 0.0 for q in "VSPGYN"}, {q: set() for q in "VSPGYN"}
        for i in range(n):
            if not left[i]:
                pool[ops[i]["q"]].add(i)
        done = []
        while len(done) < n:
            best = None
            for q, c in pool.items():
                if not c:
                    continue
                f = free[q] if q != "N" else 0.0
                top = max(c, key=lambda i: (prio[i], -i))
                lim = max(f, rdy[top]) + slack
                fit = [i for i in c if q == "V" and i < top + 30 and max(f, rdy[i]) + ops[i]["us"] <= lim]
                pick = min(fit, key=lambda i: (max(f, rdy[i]), -prio[i], i)) if fit and rdy[top] > f else top
                s = max(f, rdy[pick])
                if best is None or s < best[0]:
                    best = (s, q, pick)
            s, q, i = best
            pool[q].discard(i)
            start[i], end[i] = s, s + ops[i]["us"]
            free[q] = end[i]
            done.append(i)
            for j in succ[i]:
                left[j] -= 1
                rdy[j] = max(rdy[j], end[i] + lat)
                if not left[j]:
                    pool[ops[j]["q"]].add(j)
        for i in done:
            o = ops[i]
            q = o["q"]
            if o["kind"] == "land":
                continue
            deps = {}
            for d in o["deps"]:
                a, b = ops[d]["sig"]
                deps[a] = max(deps.get(a, 0), b)
            for a in sorted(deps, key=lambda a: a == "q" + q):
                require(q, (a, deps[a]))
            if o["kind"] == "call":
                a = "q" + q
                for c in o["calls"]:
                    c().then_inc(T.sem[a], 1)
                    cnt[a] = cnt.get(a, 0) + 1
                o["sig"] = (a, cnt[a])
                snap[o["sig"]] = dict(seen[q])
            else:
                o["calls"]()

    def X(name, idx=None, tok=None, n=256):
        return (T[name][:] if idx is None else T[name][idx], tok or name, n)

    def cols(name, a, b, tok=None):
        return X(name, (slice(None), slice(a, b)), tok, b - a)

    lanes = {"LF": {}, "LI": {}}

    def lane(buf, n):
        j = lanes[buf].setdefault(n, len(lanes[buf]))
        return cols(buf, 16 * j, 16 * j + 16, buf + ":" + n)

    def F(n):
        return lane("LF", n)

    def I(n):
        return lane("LI", n)

    def first(name):
        return X(name, (slice(None), slice(0, 256, 16)), None, 16)

    def final(name):
        return X(name, (slice(None), slice(15, 256, 16)), None, 16)

    def cyc(n):
        return max(64, n) * 0.83e-3

    v, s_, p = g.vector, g.scalar, g.tensor

    def tt(o, a, b, op):
        do("V", [a[1], b[1]], [o[1]], [lambda: v.tensor_tensor(out=o[0], in0=a[0], in1=b[0], op=op)],
           cyc(o[2] * (1 if {a[1].split(":")[0], b[1].split(":")[0]} & banks else 2)))

    def ts(o, a, s1, op0, s2=None, op1=None, extra=()):
        kw = {"op1": op1} if op1 is not None else {}
        do("V", [a[1]] + list(extra), [o[1]],
           [lambda: v.tensor_scalar(out=o[0], in0=a[0], scalar1=s1, scalar2=s2, op0=op0, **kw)], cyc(o[2]))

    def cp(o, a):
        do("V", [a[1]], [o[1]], [lambda: v.tensor_copy(out=o[0], in_=a[0])], cyc(o[2]))

    def fill(o, c):
        do("V", [], [o[1]], [lambda: v.memset(o[0], c)], 0.2 if o[1] != "SELC" else 0.9)

    def scan(o, d0, d1, op0, op1):
        do("V", [d0[1], d1[1]], [o[1]],
           [lambda: v.tensor_tensor_scan(out=o[0], data0=d0[0], data1=d1[0], initial=0.0, op0=op0, op1=op1)], cyc(o[2]))

    def act(o, a, func, scale=1.0, bias=0.0, extra=()):
        do("S", [a[1]] + list(extra), [o[1]], [lambda: s_.activation(out=o[0], in_=a[0], func=func, scale=scale, bias=bias)],
           cyc(o[2]) if o[1] != "SELS" else 1.7)

    def mm(o, pairs):
        reads = [t[1] for pr in pairs for t in pr]
        n = len(pairs)
        do("P", reads, [o[1]], [(lambda i=i, l=l, r=r: p.matmul(o[0], l[0], r[0], i == 0, i == n - 1)) for i, (l, r) in enumerate(pairs)],
           n * max(64, o[2]) * 0.42e-3)

    SHR, AND = A.logical_shift_right, A.bitwise_and

    def load(q, name, dst):
        s = "ld_" + name
        cnt[s] = 16
        eng[q].dma_start(dst[0], T[name][:]).then_inc(T.sem[s], 16)
        do("N", [], [dst[1]], [], 4.5 if name == "prop" else 2.3, "land")["sig"] = (s, 16)
    load("Y", "con", X("conA"))
    load("S", "prop", cols("P", 0, 2048))
    load("Y", "ex", X("yv"))
    load("Y", "lem", X("lemA"))
    load("Y", "org", X("orgA"))
    load("Y", "cnt", X("cntA"))
    load("Y", "lim", X("limA"))

    def sel(o, a, pat, cmp, fillv, base, cm):
        do("G", [a[1]], [o[1]], [lambda: g.affine_select(o[0], a[0], pat, cmp, fillv, base, cm)], 0.17 + 2 * cyc(o[2]))

    def iota(o, pat, base, cm):
        do("G", [], [o[1]], [lambda: g.iota(o[0], pat, base, cm, allow_small_or_imprecise_dtypes=True)], 0.13 + 2 * cyc(o[2]))
    fill(X("ones"), 1.0)
    one128 = cols("ones", 0, 128)
    sel(X("ID"), one128, [[-1, 128]], A.is_equal, 0.0, 0, 1)
    sel(X("BT"), one128, [[-16, 8], [0, 16]], A.is_ge, 0.0, 0, 1)
    sel(X("BLK"), X("BT"), [[16, 8], [0, 16]], A.is_ge, 0.0, 15, -1)
    fill(cols("P", 2048, 2304, "Pz"), 0.0)
    fill(X("THR"), 9.5 * BIG)
    fill(X("SELC"), 0.0)
    fill(X("EVC"), 0.0)
    fill(X("EVL"), 0.0)
    fill(X("ERC"), -1.0)
    fill(X("ERL"), -1.0)
    fill(X("fb"), -float(2 ** 30))
    fill(X("SC"), 1.0)
    fill(I("w"), 0)
    emp = X("f0")
    ts(emp, X("conA"), 0.0, A.is_lt)
    ts(X("f1"), emp, 2049.0, A.mult)
    tt(X("f1"), X("f1"), X("conA"), A.add)
    cp(cols("C16", 0, 256, "C16_0"), X("f1"))
    mm(X("pY", (slice(None), slice(0, 16))), [(X("ID"), X("yv"))])
    cp(cols("L16", 0, 256, "L16_0"), X("lemA"))
    do("V", ["BLK"], ["SELC"],
       [(lambda i=i: v.tensor_scalar(out=T.SELC[:, 129 * i:128 * i + 128:16], in0=T.BLK[:, 0:128:16], scalar1=-BIG, scalar2=None,
                                     op0=A.mult)) for i in range(16)], 0.9)

    def selq(nm, q):
        return cols(nm, 128 * q, 128 * q + 128, nm)
    yr = [X("yv", (slice(None), slice(q, 256, 16))) for q in range(16)]

    def gather(t, lst, dst, m, q="S"):
        tok = "%s_%d" % (lst, t)
        win = T.P[:, 0:2064].indirect(T[lst][:, 256 * t + 16 * m:256 * t + 16 * m + 16])
        out = T[dst][:, m, :]
        do(q, [tok, "P", "Pz"], ["%s:%d" % (dst, m)],
           [(lambda: s_.activation(out=out, in_=win, func=AF.Copy)) if q == "S" else (lambda: v.tensor_copy(out=out, in_=win))], 0.39)

    def rows_of(t, k):
        return slice(k, 256, 16) if t == 0 else slice(16 * k, 16 * k + 16)

    def lanes_of(t, q):
        return slice(16 * q, 16 * q + 16) if t == 0 else slice(q, 256, 16)

    def toks(b, m0, m1):
        return ["%s:%d" % (b, m) for m in range(m0, m1)]

    def compare(t, src, dst, op, m0, m1):
        ms = slice(m0, m1)
        do("V", toks(src, m0, m1) + ["pY"], toks(dst, m0, m1),
           [(lambda k=k: v.tensor_tensor(out=T[dst][:, ms, rows_of(t, k)], in0=T[src][:, ms, rows_of(t, k)], in1=T.pY[:, ms, :], op=op))
            for k in range(16)], 16 * cyc(16 * (m1 - m0)))

    def sums(t, src, bank, sl, const, m0, m1, made=None):
        ms, cs = slice(m0, m1), slice(16 * m0, 16 * m1)
        out = T[bank][:, cs]
        calls = [lambda: p.matmul(out, T.ID[:], T[const][:, cs], True, False)]
        calls += [(lambda q=q: p.matmul(out, T[sl][:, 128 * q:128 * q + 128], T[src][:, ms, lanes_of(t, q)], False, q == 15)) for q in range(16)]
        do("P", ["ID", const, sl] + (made or toks(src, m0, m1)), ["%s:%d" % (bank, m) for m in range(m0, m1)], calls,
           17 * max(64, 16 * (m1 - m0)) * 0.42e-3)

    def whole(bank):
        return [("%s:%d" % (bank, m)) for m in range(16)]

    def keyed(o, bank, b):
        do("V", whole(bank) + [b[1]], [o[1]], [lambda: v.tensor_tensor(out=o[0], in0=T[bank][:, 0:256], in1=b[0], op=A.max)], cyc(256))

    cpieces = [(0, 8), (8, 16)]
    HB = 4
    lpieces = [(0, 4), (4, 8), (8, 12), (12, 16)]
    VG = 3
    dst = T.cores[(rank + HOP) % len(T.cores)]
    rid, pid = topo.addr(dst, core)
    msk = topo.mask(core, dst)
    neng = len(topo.engines(core, dst))
    sent = [0]

    def send(kind, t):
        c = slice(256 * t, 256 * t + 256)
        d = slice(256 * t + 256, 256 * t + 512)
        a = "a%s_%d" % (kind, t + 1)
        do("G", ["o%s_%d" % (kind, t)], ["net" + a],
           lambda: g.remote_dma(T[kind][:, d], T["o" + kind][:, c], T.sem[a], T.sem.sent, pid, rid, msk), 0.8, "send")
        do("N", ["net" + a], ["%s_%d" % (kind, t + 1)], [], 3.0, "land")["sig"] = (a, neng)
        sent[0] += neng

    def masks(src, y):
        for e in range(2):
            act(X(y, (slice(None), slice(None), slice(16 * e, 16 * e + 16)), "%s%d" % (y, e)), src, AF.Copy, T.col[:, e:e + 1], extra=["col"])

    def turn(y, dst):
        do("V", [y + "0", y + "1"], ["Z"], [(lambda m=m: v.transpose(out=T.Z[:, m, :], in_=T[y][:, m, :])) for m in range(16)], 0.85)
        tt(dst, X("Z", (slice(None), slice(None), slice(0, 16))), X("Z", (slice(None), slice(None), slice(16, 32))), A.add)

    def consts():
        tt(cols("mt", 0, 64), cols("ID", 0, 64), cols("ID", 64, 128), A.add)
        tt(cols("mt", 64, 96), cols("mt", 0, 32), cols("mt", 32, 64), A.add)
        tt(cols("RK", 0, 16), cols("mt", 64, 80), cols("mt", 80, 96), A.add)
        for w in (16, 32, 64, 128):
            cp(cols("RK", w, 2 * w), cols("RK", 0, w))
        tt(X("kq"), cols("RK", 0, 16), cols("KI", 0, 16), A.mult)
        do("V", ["kq"], ["col"], [lambda: v.tensor_reduce(out=T.col[:, 2:3], in_=T.kq[:], axis=AX.X, op=A.add)])
        do("V", ["BLK"], ["col"], [lambda: v.tensor_reduce(out=T.col[:, 0:1], in_=T.BLK[:, 0:128:32], axis=AX.X, op=A.add)])
        ts(X("col", (slice(None), slice(1, 2))), X("col", (slice(None), slice(0, 1))), -1.0, A.mult, 1.0, A.add)
        ts(X("col", (slice(None), slice(3, 4))), X("col", (slice(None), slice(2, 3))), float(2 ** 20), A.mult)
        ts(X("col", (slice(None), slice(4, 5))), X("col", (slice(None), slice(2, 3))), 65536.0, A.mult, 65536.0, A.add)
        ts(X("cb"), X("cb"), T.col[:, 2:3], A.add, extra=["col"])
        ts(X("pY", (slice(None), slice(16, 32)), "pY:k"), X("KI"), 0.0625, A.mult)
        ts(X("NID"), X("ID"), -1.0, A.mult)
        cp(X("D1h"), X("D1"))
        ts(X("limf"), X("limA"), 16384.0, A.mult)

    def pack():
        ts(X("f2"), X("f1"), 8.0, A.mult, T.col[:, 3:4], A.add, extra=["col"])
        ts(X("f4"), X("orgA"), 65536.0, A.mult)
        ts(X("f3"), emp, 7.0, A.mult, 1.0, A.add)
        tt(X("f2"), X("f2"), X("f4"), A.add)
        tt(X("f4"), X("f3"), X("cntA"), A.mult)
        ts(X("f3"), X("lemA"), 8.0, A.mult, T.col[:, 4:5], A.add, extra=["col"])
        tt(X("f2"), X("f2"), X("f4"), A.add)

    iota(cols("KI", 0, 256), [[0, 16], [1, 16]], 0, 0)
    iota(X("KB"), [[0, 16], [1, 16]], 0, 0)
    iota(X("cb"), [[16, 16]], 0, 0)
    sel(X("D0"), X("fb"), [[0, 16], [1, 16]], A.is_gt, float(2 ** 30), 0, 0)
    sel(X("D1"), X("SC"), [[0, 16], [1, 16]], A.is_gt, 0.0, 0, 0)

    def u_sum(t):
        mm(cols("pM", 0, 16, "pM:u"), [(selq("SELS", q), yr[q]) for q in range(16)])
        act(F("u"), cols("pM", 0, 16, "pM:u"), AF.Copy, 1.0 / 16)
        act(F("u32"), cols("pM", 0, 16, "pM:u"), AF.Identity, 1.0 / 512, 1.0)
        act(F("v37"), cols("pM", 0, 16, "pM:u"), AF.Identity, 37.0 / 16, float(t))

    def update(e_row, e_val, R, e, at, old, new):
        pa, pb = cols("pT", 0, 256, "pT:a"), cols("pT", 256, 512, "pT:b")
        scan(X(R), X("D1h"), X(e_row), A.mult, A.add)
        scan(pa, X("D1"), X(e_val), A.mult, A.add)
        ts(X(e), X(R), at, A.is_equal)
        tt(pb, pa, old, A.subtract)
        tt(pa, pb, X(e), A.mult)
        tt(new, pa, old, A.add)

    stores = [0]

    def store(q, name, src):
        do(q, [src[1]], [], lambda: eng[q].dma_start(T[name][:], src[0]).then_inc(T.sem.outs, 16), 0.1, "store")
        stores[0] += 16

    for t in range(TV):
        last = t == TV - 1
        c0, c1 = 256 * t, 256 * t + 256
        pk, lk = cols("PK", c0, c1, "PK_%d" % t), cols("LK", c0, c1, "LK_%d" % t)
        opk, olk = cols("oPK", c0, c1, "oPK_%d" % t), cols("oLK", c0, c1, "oLK_%d" % t)
        if last:
            opk, olk = X("zPK"), X("zLK")
        if t == 0:
            consts()
            ts(cols("RLM", 0, 256, "RLM_0"), X("RK"), T.limf[:, 0:1], A.mult, extra=["limf"])
        for m in range(16):
            gather(t, "C16", "PC", m, "V" if m < VG else "S")
        def conditions(m0, m1):
            compare(t, "PC", "XC", A.is_gt, m0, m1)
            sums(t, "XC", "pC", "SELC", "THR", m0, m1)

        def lemma(m0, m1):
            if m0 < HB:
                compare(t, "PL", "DL", A.subtract, m0, m1)
                do("V", toks("DL", m0, m1), toks("XL", m0, m1),
                   [lambda: v.tensor_scalar(out=T.XL[:, m0:m1, :], in0=T.DL[:, m0:m1, :], scalar1=0.0, scalar2=None, op0=A.is_gt)],
                   cyc(128 * (m1 - m0)))
            else:
                compare(t, "PL", "XL", A.is_gt, m0, m1)
            sums(t, "XL", "pL", "SELC", "THR", m0, m1)
        for m in range(16 if t else 8):
            gather(t, "L16", "PL", m)
        if t == 0:
            conditions(*cpieces[0])
            pack()
            masks(X("f2"), "Yp")
            masks(X("f3"), "Yl")
            for m in range(8, 16):
                gather(t, "L16", "PL", m)
            act(X("SELS"), X("SELC"), AF.Copy, -16.0 / BIG)
            conditions(*cpieces[1])
            turn("Yp", cols("PK", 0, 256, "PK_0"))
            lemma(*lpieces[0])
            turn("Yl", cols("LK", 0, 256, "LK_0"))
            lemma(*lpieces[1])
            u_sum(0)
        lp = cols("pM", 256, 512, "pM:l")
        mm(lp, [(X("BLK"), cols("RLM", c0, c1, "RLM_%d" % t))])
        x, sl = X("i0"), I("sl")
        ts(x, pk, 0x4007, AND)
        tt(X("KC"), lp, pk, A.add)
        tt(X("keyS"), X("pY", (slice(None), slice(16, 32)), "pY:k"), x, A.subtract)
        scan(X("SS"), X("D0"), X("keyS"), A.max, A.min)
        ts(sl, final("SS"), 16.0, A.mult)
        ts(sl, sl, 15, AND)
        ts(F("sP"), sl, float(2 ** 20), A.mult, -65536.0, A.add)
        if t:
            for m0, m1 in cpieces:
                conditions(m0, m1)
            lemma(*lpieces[0])
        keyed(X("key"), "pC", X("KC"))
        scan(X("SB"), X("D0"), X("key"), A.max, A.min)
        mb, mi = final("SB"), I("mi")
        ts(X("bfl"), mb, CAP, A.is_lt)
        ts(mi, mb, CAP + 49152.0, A.min)
        ts(I("lim"), mi, 14, SHR, 3, AND)
        ts(I("b"), mi, 7, AND)
        ts(I("t2"), mi, 0x3FFF, AND)
        ts(I("t1"), mi, 0x1FF0000, AND)
        tt(F("bl"), I("b"), I("lim"), A.subtract)
        ts(F("t2p"), I("t2"), 1.0, A.add)
        ts(I("vb"), mi, 0x0F3FF8, AND)
        tt(F("ov"), F("bl"), I("w"), A.is_ge)
        ts(F("vb1"), I("vb"), 65536.0, A.add)
        ts(F("tb"), mb, CAP, A.is_lt, 2 * CAP, A.mult)
        ts(F("o14"), F("ov"), 16384.0, A.mult)
        tt(F("vB"), F("vb1"), F("ov"), A.mult)
        tt(F("z"), F("o14"), F("t2p"), A.max)
        tt(F("nb"), F("z"), I("t1"), A.add)
        if not last:
            mm(cols("pM", 16, 32, "pM:w"), [(cols("RK", 0, 128), X("bfl"))])
        for m0, m1 in lpieces[1 if t else 2:]:
            lemma(m0, m1)
        do("S", toks("DL", 0, HB), toks("AB", 0, HB),
           [lambda: s_.activation(out=T.AB[:, 0:HB, :], in_=T.DL[:, 0:HB, :], func=AF.Abs)], cyc(256 * HB))
        for kk in range(8):
            bank = "pD%d" % (kk % 2)
            calls = []
            for j in range(2):
                o = T[bank][:, HB:16, 16 * j:16 * j + 16]
                calls.append(lambda o=o, r=rows_of(t, 2 * kk + j): p.matmul(o, T.ID[:], T.PL[:, HB:16, r], True, False))
                calls.append(lambda o=o: p.matmul(o, T.NID[:], T.yv[:, 16 * HB:256], False, True))
            do("P", ["ID", "NID", "yv"] + toks("PL", HB, 16), [bank], calls, 4 * 16 * (16 - HB) * 0.42e-3)
            do("S", [bank], toks("AB%d" % kk, HB, 16),
               [lambda kk=kk, bank=bank: s_.activation(out=T.AB[:, HB:16, 32 * kk:32 * kk + 32], in_=T[bank][:, HB:16, :], func=AF.Abs)],
               cyc(32 * (16 - HB)))
        sums(t, "AB", "pS", "SELS", "KB", 0, HB)
        sums(1, "AB", "pS", "SELS", "KB", HB, 16, [x for kk in range(8) for x in toks("AB%d" % kk, HB, 16)])
        if not last:
            act(cols("RLM", c1, c1 + 256, "RLM_%d" % (t + 1)), X("RK"), AF.Copy, T.limf[:, t + 1:t + 2], extra=["limf"])
        tt(I("uu"), F("u"), F("u"), A.mult)
        ts(I("uu"), I("uu"), 5, SHR)
        tt(I("fs"), I("uu"), F("v37"), A.add)
        ts(I("fs"), I("fs"), 2047, AND)
        ts(F("new8"), I("fs"), 8.0, A.mult, 65536.0, A.add)
        if not last:
            cp(I("w"), cols("pM", 16, 32, "pM:w"))
            ts(I("w"), I("w"), 3, AND)
        keyed(X("key"), "pL", lk)
        scan(X("SG"), X("D0"), X("key"), A.max, A.min)
        mg = final("SG")
        tt(F("ng"), F("sP"), mg, A.add)
        tt(F("q"), F("ng"), F("tb"), A.max)
        tt(I("vc"), F("q"), F("nb"), A.min)
        ts(I("gq"), F("q"), CAP + 16384.0, A.min)
        ts(I("kc"), I("vc"), 20, SHR)
        cp(first("EVC"), I("vc"))
        cp(first("ERC"), I("kc"))
        ts(I("al"), I("gq"), 3, SHR, 4095, AND)
        update("ERC", "EVC", "RC", "eC", 0.0, pk, opk)
        if not last:
            ts(X("i1"), opk, 3, SHR, 4095, AND)
            cp(cols("oC16", c0, c1, "oC16_%d" % t), X("i1"))
            send("C16", t)
            send("PK", t)
        cp(cols("U16", 0, 16, "a16"), I("al"))
        tt(F("x"), F("u32"), I("al"), A.mult)
        ts(F("cg"), I("al"), 2048.0, A.is_ge, 2304.0, A.mult)
        ts(I("h"), F("x"), 97.0 * t - 131072.0 - 31.0 / 64, A.add)
        do("V", ["P", "Pz", "a16", "yv"], ["mn"],
           [lambda: v.tensor_tensor(out=T.mn[:], in0=T.P[:, 0:2064].indirect(T.U16[:, 0:16]), in1=T.yv[:], op=A.min)], 0.4)
        ts(I("h"), I("h"), 1792, AND)
        tt(F("cg"), F("cg"), X("cb"), A.add)
        tt(F("n"), I("h"), F("cg"), A.add)
        cp(cols("U16", 16, 32, "n16"), F("n"))
        do("V", ["P", "Pz", "a16", "yv"], ["dv"],
           [lambda: v.tensor_tensor(out=T.dv[:], in0=T.P[:, 0:2064].indirect(T.U16[:, 0:16]), in1=T.yv[:], op=A.subtract)], 0.4)
        do("V", ["mn", "n16"], ["P"],
           [lambda: v.tensor_copy(out=T.P[:, 0:4352].indirect(T.U16[:, 16:32]), in_=T.mn[:])], 0.7)
        act(X("yv"), X("dv"), AF.Abs)
        if not last:
            mm(X("pY", (slice(None), slice(0, 16))), [(X("ID"), X("yv"))])
            u_sum(t + 1)
        if last:
            masks(opk, "Yp")
            store("Y", "zp", cols("P", 0, 2048))
            store("Y", "zy", X("yv"))
            turn("Yp", X("i0"))
            ts(X("i1"), X("i0"), 3, SHR, 4095, AND)
            ts(X("i2"), X("i0"), 7, AND)
            ts(X("f0"), X("i1"), 2048.0, A.is_ge)
            ts(X("f2"), X("i1"), -2048.0, A.add)
            ts(X("f0"), X("f0"), -4097.0, A.mult, 4096.0, A.add)
            tt(X("h0"), X("f2"), X("i2"), A.max)
            tt(X("f1"), X("i1"), X("f0"), A.min)
            ts(X("i2"), X("i0"), 16, SHR, 15, AND)
            store("Y", "zb", X("h0"))
            store("Y", "zc", X("f1"))
            cp(X("h1"), X("i2"))
            store("Y", "zo", X("h1"))
        do("V", whole("pS") + ["D0"], ["SC"],
           [lambda: v.tensor_tensor_scan(out=T.SC[:], data0=T.D0[:], data1=T.pS[:, 0:256], initial=0.0, op0=A.max, op1=A.min)], cyc(256))
        cp(I("ks"), final("SC"))
        ts(I("gk"), I("gq"), 0x0F0000, AND)
        ts(F("n8"), F("n"), 8.0, A.mult, 65536.0, A.add)
        ts(I("ks"), I("ks"), 15, AND)
        ts(F("gf"), F("q"), CAP, A.is_lt)
        tt(F("vG"), F("n8"), I("gk"), A.add)
        ts(F("k16"), I("ks"), 65536.0, A.mult)
        ts(F("cf"), I("vc"), CAP, A.is_ge)
        tt(F("vG"), F("vG"), F("gf"), A.mult)
        tt(F("vC"), F("k16"), F("new8"), A.add)
        tt(F("vG"), F("vG"), F("vB"), A.max)
        tt(F("vC"), F("vC"), F("cf"), A.mult)
        tt(I("vl"), F("vG"), F("vC"), A.max)
        ts(I("rl"), I("vl"), 16, SHR)
        cp(first("EVL"), I("vl"))
        cp(first("ERL"), I("rl"))
        update("ERL", "EVL", "RL", "eL", 1.0, lk, olk)
        if not last:
            ts(X("i2"), olk, 3, SHR, 2047, AND)
            cp(cols("oL16", c0, c1, "oL16_%d" % t), X("i2"))
            send("L16", t)
            send("LK", t)

    masks(X("zLK"), "Yl")
    turn("Yl", X("i0"))
    ts(X("i1"), X("i0"), 3, SHR, 2047, AND)
    cp(X("f3"), X("i1"))
    store("Y", "zl", X("f3"))
    emit()
    g.sync.wait_ge(T.sem.outs, stores[0])
    g.wait_ge(T.sem.sent, sent[0])
    for s in cnt:
        g.wait_ge(T.sem[s], cnt[s])
